import numpy as np
import ml_dtypes


def mxq(x, axis, fmt="e4m3"):
    dtype, down = {"e4m3": (ml_dtypes.float8_e4m3fn, 7), "e5m2": (ml_dtypes.float8_e5m2, 14)}[fmt]
    v = np.moveaxis(np.asarray(x, np.float32).astype(ml_dtypes.bfloat16).astype(np.float64), axis, -1)
    blocks = v.reshape(v.shape[:-1] + (-1, 32))
    amax = np.abs(blocks).max(-1, keepdims=True)
    byte = np.maximum(np.where(amax > 0, np.frexp(amax)[1] - 1 + 127, 0) - down, 1)
    scale = np.exp2(byte - 127.0)
    codes = (blocks / scale).astype(np.float32).astype(dtype).astype(np.float64)
    return np.moveaxis((codes * scale).reshape(v.shape), -1, axis)


WIDE = False


def mx_kscale(k):
    if not WIDE:
        return np.ones(k)
    levels = np.array([10, -10, 5, -5, 0])
    if k % 512:
        return np.exp2(np.random.permutation(np.resize(levels, k // 32))).repeat(32)
    a = np.empty((k // 512, 16))
    for p in range(k // 512):
        a[p, :8] = np.random.permutation(np.resize(levels, 8))
        for g in range(8):
            far = levels[np.abs(levels - a[p, g]) >= 10]
            a[p, g + 8] = far[np.random.randint(len(far))]
    return np.exp2(a.ravel()).repeat(32)


BF16 = ml_dtypes.bfloat16


def bf(x):
    return np.asarray(x, np.float32).astype(BF16)


def f64(x):
    return np.asarray(x).astype(np.float64)


E2M1 = np.array([0.0, 0.5, 1.0, 1.5, 2.0, 3.0, 4.0, 6.0, -0.0, -0.5, -1.0, -1.5, -2.0, -3.0, -4.0, -6.0])


def pack_weight(w, fmt):
    k, n = w.shape
    w = f64(bf(w)).reshape(k // 32, 32, n)
    amax = np.abs(w).max(1)
    if fmt == "e4m3":
        byte = np.frexp(amax)[1] - 1 + 127 - 7
    else:
        mant, ex = np.frexp(amax / 6.0)
        byte = np.where(mant > 0.5, ex, ex - 1) + 127
    byte = np.clip(np.where(amax > 0, byte, 1), 1, 254)
    scaled = (w * np.exp2(127.0 - byte)[:, None, :]).reshape(k, n).astype(np.float32)
    by_word = np.ascontiguousarray(scaled.reshape(k // 512, 128, 4, n).transpose(0, 1, 3, 2))
    if fmt == "e4m3":
        words = by_word.astype(ml_dtypes.float8_e4m3fn).view(np.uint8)
    else:
        c = by_word.astype(ml_dtypes.float4_e2m1fn).view(np.uint8) & 0xF
        words = c[..., 0::2] | (c[..., 1::2] << 4)
    return np.ascontiguousarray(words), np.ascontiguousarray(byte.astype(np.uint8).reshape(k // 512, 16, n))


def unpack_weight(words, scales, fmt):
    g, p, n, _ = words.shape
    if fmt == "e4m3":
        vals = np.ascontiguousarray(words).view(ml_dtypes.float8_e4m3fn).astype(np.float64)
    else:
        nib = np.empty((g, p, n, 4), np.uint8)
        nib[..., 0::2] = words & 0xF
        nib[..., 1::2] = words >> 4
        vals = E2M1[nib]
    vals = vals * np.repeat(np.exp2(scales.astype(np.float64) - 127.0), 8, axis=1)[..., None]
    return vals.transpose(0, 1, 3, 2).reshape(g * 512, n)
def pack4(w):
    words, scales = pack_weight(w, "e2m1")
    return words.reshape(words.shape[0], 128, -1), scales


def unpack4(words, scales):
    return unpack_weight(words.reshape(words.shape[0], 128, -1, 2), scales, "e2m1")


def planes(Y):
    n, m = Y.shape
    b = f64(bf(Y)).reshape(n // 32, 32, m)
    amax = np.abs(b).max(1)
    byte = np.clip(np.where(amax > 0, np.frexp(amax)[1] - 1 + 127 - 7, 1), 1, 254)
    codes = (b * np.exp2(127.0 - byte)[:, None, :]).reshape(n, m).astype(np.float32).astype(ml_dtypes.float8_e4m3fn).view(np.uint8)
    words = codes.reshape(n // 512, 128, 4, m).transpose(0, 1, 3, 2)
    return np.ascontiguousarray(words), np.ascontiguousarray(byte.astype(np.uint8).reshape(n // 512, 16, m))


R, Z, N, C = 1024, 512, 1024, 2048
STEP = 0.33
RHO = 0.3

def setup_inputs():
    rn = np.random.randn
    s, t, u = mx_kscale(Z), mx_kscale(N), mx_kscale(C)
    z = rn(R, Z) * s
    B = STEP * rn(Z, N) / np.sqrt(Z) / s[:, None] * t
    z_words, z_scales = pack_weight(z.T, "e4m3")
    B_words, B_scales = pack4(B)
    return {
        "z_words": z_words, "z_scales": z_scales,
        "B_words": B_words, "B_scales": B_scales,
        "x0": bf(rn(R, N) * t),
        "A": bf(rn(C, N) / np.sqrt(N) / (u[:, None] * t)),
        "b": bf(0.5 * rn(C) / u),
        "lam": bf(np.abs(rn(R, C)) * u),
        "rho": bf(RHO * np.exp(0.2 * rn(C)) * u * u),
        "d": bf(0.5 * np.exp(0.8 * rn(N)) * t),
    }

def reference(z_words, z_scales, B_words, B_scales, x0, A, b, lam, rho, d):
    zt = unpack_weight(z_words, z_scales, "e4m3")
    B = unpack4(B_words, B_scales)
    A = f64(A)
    w = f64(x0) + (zt.T @ B)
    v = mxq(w, 1) @ mxq(A, 1).T
    mu = np.maximum(f64(lam) + f64(rho) * (v - f64(b)), 0.0)
    y = f64(d) * (mxq(mu, 1) @ mxq(A, 0))
    Y = y.T
    words, scales = planes(Y)
    return y, words, scales

@@ -1,0 +1,516 @@
+from contextlib import ExitStack
+
+import concourse.mybir as mybir
+from concourse.masks import make_identity
+
+R, Z, N, C = 1024, 512, 1024, 2048
+FLOPS = 2 * R * Z * N + 2 * 2 * R * N * C
+
+F32 = mybir.dt.float32
+BF16 = mybir.dt.bfloat16
+I32 = mybir.dt.int32
+U32 = mybir.dt.uint32
+U8 = mybir.dt.uint8
+FP8X4 = mybir.dt.float8_e4m3fn_x4
+FP4X4 = mybir.dt.float4_e2m1fn_x4
+ALU = mybir.AluOpType
+ACT = mybir.ActivationFunctionType
+
+P = 128
+K = 512
+N_PASSES = N // K
+C_PASSES = C // K
+BANKS = 6
+
+
+def tile_augmented_lagrangian_inequality_grad_k1_kernel(
+    tc, z_words, z_scales, B_words, B_scales, x0, A, b, lam, rho, d, out_0, out_1, out_2
+):
+    nc = tc.nc
+    with ExitStack() as ctx:
+        keep = ctx.enter_context(tc.tile_pool(name="keep", bufs=1))
+        ring = ctx.enter_context(tc.tile_pool(name="ring", bufs=2))
+        psum = ctx.enter_context(tc.psum_pool(name="psum", bufs=1))
+        ctx.enter_context(tc.manual_schedule())
+
+        t = {}
+        bank_count = [0]
+
+        def next_bank():
+            tag = "bank%d" % (bank_count[0] % BANKS)
+            bank_count[0] = bank_count[0] + 1
+            return psum.tile([P, K], F32, name=tag, tag=tag)
+
+        def kept(name, shape, dtype):
+            return keep.tile(shape, dtype, name=name, tag=name, align_bytes=64)
+
+        def ringed(name, shape, dtype, bufs):
+            return ring.tile(shape, dtype, name=name, tag=name, bufs=bufs, align_bytes=64)
+
+        ident = kept("ident", [P, P], F32)
+        z_plane = kept("z_plane", [P, R], U8)
+        b_codes = kept("b_codes", [P, 2 * N], U8)
+        b_plane = kept("b_plane", [P, N], U8)
+        rho_bf = kept("rho_bf", [P, 16], BF16)
+        rhs_bf = kept("rhs_bf", [P, 16], BF16)
+        rho_f = kept("rho_f", [P, 16], F32)
+        shift = kept("shift", [P, 16], F32)
+        d_row = kept("d_row", [P, N], BF16)
+        warm = kept("warm", [P, 8], F32)
+
+        def load_a(g, half):
+            if half == 0:
+                t["a", g] = kept("a_raw%d" % g, [P, 4 * N], BF16)
+            cols = slice(2 * N * half, 2 * N * (half + 1))
+            rows = A[K * g : K * (g + 1), :].rearrange("(p j) n -> p (j n)", j=4)
+            nc.sync.dma_start(out=t["a", g][:, cols], in_=rows[:, cols])
+
+        def load_a_whole(g):
+            t["a", g] = kept("a_raw%d" % g, [P, 4 * N], BF16)
+            rows = A[K * g : K * (g + 1), :].rearrange("(p j) n -> p (j n)", j=4)
+            nc.sync.dma_start(out=t["a", g][:], in_=rows)
+
+        def load_plane(queue, plane, rows, quadrants):
+            for q in quadrants:
+                queue.dma_start(
+                    out=plane[32 * q : 32 * q + 4, :].bitcast(I32), in_=rows[0, 4 * q : 4 * q + 4, :].bitcast(I32)
+                )
+
+        def load_x0(i):
+            t["x0", i] = ringed("x0", [P, N], BF16, 5)
+            nc.sync.dma_start(out=t["x0", i][:], in_=x0[P * i : P * (i + 1), :])
+
+        def load_lam(step):
+            ch, half = divmod(step, 2)
+            t["lam", step] = ringed("lam", [P, 2 * 1024], BF16, 4)
+            rows = lam[2 * P * ch : 2 * P * (ch + 1), 1024 * half : 1024 * (half + 1)].rearrange("(i p) c -> p i c", p=P)
+            nc.sync.dma_start(out=t["lam", step][:].rearrange("p (i c) -> p i c", i=2), in_=rows)
+
+        def at_turn(g, j):
+            words = t["a", g][:].bitcast(F32)
+            bank = t["at_bank", g, j] = next_bank()
+            for h in range(N_PASSES):
+                for u in range(2):
+                    first = 512 * j + 256 * h
+                    nc.tensor.transpose(
+                        bank[:, P * (2 * h + u) : P * (2 * h + u + 1)], words[:, first + u : first + 256 : 2], ident[:]
+                    )
+
+        def at_copy(g, j):
+            t["at_bf", g, j] = ringed("at_bf", [P, K], F32, 4)
+            nc.scalar.copy(
+                out=t["at_bf", g, j][:].rearrange("p (h c u) -> p h c u", h=2, u=2),
+                in_=t["at_bank", g, j][:].rearrange("p (h u c) -> p h c u", h=2, u=2),
+            )
+
+        def at_quant(g, j):
+            t["at_codes", g, j] = kept("at_codes%d_%d" % (g, j), [P, 256], U32)
+            t["at_plane", g, j] = kept("at_plane%d_%d" % (g, j), [P, 256], U8)
+            nc.vector.quantize_mx(
+                out=t["at_codes", g, j][:].bitcast(FP8X4),
+                scales=t["at_plane", g, j][:],
+                in_=t["at_bf", g, j][:].bitcast(BF16),
+            )
+
+        def a_weave(piece, on_vector):
+            h, g, part = piece // 8, piece % 8 // 2, piece % 2
+            t["a_bf", piece] = ringed("a_bf", [P, 1024], BF16, 4)
+            first = K * h + 256 * part
+            src = t["a", g][:].rearrange("p (j n) -> p j n", j=4)[:, :, first : first + 256]
+            src = src.rearrange("p j (c i) -> p c j i", i=4)
+            dst = t["a_bf", piece][:].rearrange("p (c i j) -> p c j i", i=4, j=4)
+            if on_vector:
+                nc.vector.tensor_copy(out=dst, in_=src)
+            else:
+                nc.scalar.copy(out=dst, in_=src)
+
+        def a_quant(piece):
+            h, g, part = piece // 8, piece % 8 // 2, piece % 2
+            if part == 0:
+                t["a_codes", g, h] = kept("a_codes%d_%d" % (g, h), [P, K], U32)
+                t["a_plane", g, h] = kept("a_plane%d_%d" % (g, h), [P, K], U8)
+            cols = slice(256 * part, 256 * (part + 1))
+            nc.vector.quantize_mx(
+                out=t["a_codes", g, h][:, cols].bitcast(FP8X4), scales=t["a_plane", g, h][:, cols], in_=t["a_bf", piece][:]
+            )
+
+        def s1_mm(i, h):
+            bank = t["s1", i, h] = next_bank()
+            nc.tensor.matmul_mx(
+                out=bank[:],
+                lhsT=t["z", i // 4][:, P * (i % 4) : P * (i % 4 + 1)].bitcast(FP8X4),
+                lhsT_scale=z_plane[:, P * i : P * (i + 1)],
+                rhs=b_codes[:, 2 * K * h : 2 * K * (h + 1)].bitcast(FP4X4),
+                rhs_scale=b_plane[:, K * h : K * (h + 1)],
+                start=True,
+                stop=True,
+            )
+
+        def w_add(i, h):
+            if h == 0:
+                t["w_rows", i] = ringed("w_rows", [P, N], BF16, 3)
+            nc.vector.tensor_tensor(
+                out=t["w_rows", i][:, K * h : K * (h + 1)].rearrange("r (u p e) -> r u p e", u=2, e=2),
+                in0=t["s1", i, h][:].rearrange("r (p u e) -> r u p e", u=2, e=2),
+                in1=t["x0", i][:, K * h : K * (h + 1)].rearrange("r (p u e) -> r u p e", u=2, e=2),
+                op=ALU.add,
+            )
+
+        def w_turn(i):
+            words = t["w_rows", i][:].bitcast(F32)
+            bank = t["w_bank", i] = next_bank()
+            for q in range(4):
+                nc.tensor.transpose(bank[:, P * q : P * (q + 1)], words[:, P * q : P * (q + 1)], ident[:])
+
+        def w_copy(i):
+            if i % 2 == 0:
+                t["w_turned", i // 2] = ringed("w_turned", [P, 1024], F32, 2)
+            dst = t["w_turned", i // 2][:].rearrange("p (h i r u) -> p i h r u", h=2, i=2, u=2)
+            nc.scalar.copy(out=dst[:, i % 2], in_=t["w_bank", i][:].rearrange("p (h u r) -> p h r u", h=2, u=2))
+
+        def w_quant(ch):
+            t["w_codes", ch] = kept("w_codes%d" % ch, [P, K], U32)
+            t["w_plane", ch] = kept("w_plane%d" % ch, [P, K], U8)
+            nc.vector.quantize_mx(
+                out=t["w_codes", ch][:].bitcast(FP8X4), scales=t["w_plane", ch][:], in_=t["w_turned", ch][:].bitcast(BF16)
+            )
+
+        def s2_mm(unit, jj):
+            ch, g = divmod(unit, 4)
+            bank = t["s2", unit, jj] = next_bank()
+            for e in range(2):
+                for h in range(N_PASSES):
+                    cols = slice(P * h, P * (h + 1))
+                    pts = slice(256 * h, 256 * (h + 1))
+                    nc.tensor.matmul_mx(
+                        out=bank[:, 256 * e : 256 * (e + 1)],
+                        lhsT=t["at_codes", g, 2 * jj + e][:, cols].bitcast(FP8X4),
+                        lhsT_scale=t["at_plane", g, 2 * jj + e][:, cols],
+                        rhs=t["w_codes", ch][:, pts].bitcast(FP8X4),
+                        rhs_scale=t["w_plane", ch][:, pts],
+                        start=(h == 0),
+                        stop=(h == N_PASSES - 1),
+                    )
+
+        def violation(unit, jj):
+            g = unit % 4
+            if jj == 0:
+                t["viol", unit] = ringed("viol", [P, 4, 256], F32, 3)
+            for e in range(2):
+                j = 2 * jj + e
+                nc.scalar.activation(
+                    out=t["viol", unit][:, j, :],
+                    in_=t["s2", unit, jj][:, 256 * e : 256 * (e + 1)],
+                    func=ACT.Identity,
+                    bias=shift[:, 4 * g + j : 4 * g + j + 1],
+                    scale=rho_f[:, 4 * g + j : 4 * g + j + 1],
+                )
+
+        def lam_turn(unit):
+            words = t["lam", unit // 2][:].bitcast(F32)
+            tag = "lam_bank%d" % (unit % 2)
+            bank = t["lam_bank", unit] = psum.tile([P, K], F32, name=tag, tag=tag)
+            for u in range(2):
+                for i in range(2):
+                    first = 512 * i + 256 * (unit % 2)
+                    nc.tensor.transpose(
+                        bank[:, P * (2 * u + i) : P * (2 * u + i + 1)], words[:, first + u : first + 256 : 2], ident[:]
+                    )
+
+        def mu_add(unit):
+            t["mu", unit] = ringed("mu", [P, 1024], BF16, 3)
+            nc.vector.tensor_tensor(
+                out=t["mu", unit][:].rearrange("p (r u e) -> p r u e", u=2, e=2),
+                in0=t["lam_bank", unit][:].bitcast(BF16).rearrange("p (u r e) -> p r u e", u=2, e=2),
+                in1=t["viol", unit][:].rearrange("p (u e) r -> p r u e", u=2),
+                op=ALU.add,
+            )
+
+        def mu_cut(unit):
+            nc.vector.tensor_scalar_max(out=t["mu", unit][:], in0=t["mu", unit][:], scalar1=0.0)
+
+        def mu_quant(unit):
+            t["mu_codes", unit] = kept("mu_codes%d" % unit, [P, 256], U32)
+            t["mu_plane", unit] = kept("mu_plane%d" % unit, [P, 256], U8)
+            nc.vector.quantize_mx(
+                out=t["mu_codes", unit][:].bitcast(FP8X4), scales=t["mu_plane", unit][:], in_=t["mu", unit][:]
+            )
+
+        def s3_mm(i, h, passes):
+            cols = slice(P * (i % 2), P * (i % 2 + 1))
+            for g in passes:
+                if g == 0:
+                    t["s3", i, h] = next_bank()
+                unit = 4 * (i // 2) + g
+                nc.tensor.matmul_mx(
+                    out=t["s3", i, h][:],
+                    lhsT=t["mu_codes", unit][:, cols].bitcast(FP8X4),
+                    lhsT_scale=t["mu_plane", unit][:, cols],
+                    rhs=t["a_codes", g, h][:].bitcast(FP8X4),
+                    rhs_scale=t["a_plane", g, h][:],
+                    start=(g == 0),
+                    stop=(g == C_PASSES - 1),
+                )
+
+        def y_scale(i, h):
+            if i % 2 == 0:
+                t["y", i // 2, h] = ringed("y", [P, 2, K], F32, 4)
+            nc.vector.tensor_tensor(
+                out=t["y", i // 2, h][:, i % 2, :], in0=t["s3", i, h][:], in1=d_row[:, K * h : K * (h + 1)], op=ALU.mult
+            )
+
+        def y_store(pair, h):
+            dst = out_0[2 * P * pair : 2 * P * (pair + 1), K * h : K * (h + 1)].rearrange("(i p) n -> p i n", p=P)
+            nc.sync.dma_start(out=dst, in_=t["y", pair, h][:])
+
+        def y_round(i, h):
+            t["y_rows", i, h] = ringed("y_rows", [P, K], BF16, 4)
+            nc.scalar.copy(
+                out=t["y_rows", i, h][:].rearrange("r (u p e) -> r u p e", u=2, e=2),
+                in_=t["y", i // 2, h][:, i % 2, :].rearrange("r (p u e) -> r u p e", u=2, e=2),
+            )
+
+        def y_scale_round(i, h):
+            t["y_rows", i, h] = ringed("y_rows", [P, K], BF16, 4)
+            nc.vector.tensor_tensor(
+                out=t["y_rows", i, h][:].rearrange("r (u p e) -> r u p e", u=2, e=2),
+                in0=t["s3", i, h][:].rearrange("r (p u e) -> r u p e", u=2, e=2),
+                in1=d_row[:, K * h : K * (h + 1)].rearrange("r (p u e) -> r u p e", u=2, e=2),
+                op=ALU.mult,
+            )
+
+        def y_turn(i, h):
+            if i % 2 == 0:
+                t["y_bank", i // 2, h] = next_bank()
+            words = t["y_rows", i, h][:].bitcast(F32)
+            for u in range(2):
+                first = P * (2 * u + i % 2)
+                nc.tensor.transpose(t["y_bank", i // 2, h][:, first : first + P], words[:, P * u : P * (u + 1)], ident[:])
+
+        def y_copy(pair, h):
+            t["y_turned", pair, h] = ringed("y_turned", [P, K], F32, 2)
+            nc.scalar.copy(
+                out=t["y_turned", pair, h][:].rearrange("p (r u) -> p r u", u=2),
+                in_=t["y_bank", pair, h][:].rearrange("p (u r) -> p r u", u=2),
+            )
+
+        def y_quant(pair, h):
+            if ("y_codes", pair) not in t:
+                t["y_codes", pair] = kept("y_codes%d" % pair, [P, K], U32)
+            if ("y_plane", pair // 2) not in t:
+                t["y_plane", pair // 2] = kept("y_plane%d" % (pair // 2), [P, 2 * K], U8)
+            first = K * h + 256 * (pair % 2)
+            nc.vector.quantize_mx(
+                out=t["y_codes", pair][:, 256 * h : 256 * (h + 1)].bitcast(FP8X4),
+                scales=t["y_plane", pair // 2][:, first : first + 256],
+                in_=t["y_turned", pair, h][:].bitcast(BF16),
+            )
+
+        def codes_store(pair):
+            dst = out_1[:, :, 256 * pair : 256 * (pair + 1), :].rearrange("h p m t -> p h (m t)")
+            src = t["y_codes", pair][:].rearrange("p (h m) -> p h m", h=2)
+            nc.sync.dma_start(out=dst.bitcast(I32), in_=src.bitcast(I32))
+
+        def plane_store(half, queue):
+            for q in range(4):
+                dst = out_2[:, 4 * q : 4 * q + 4, K * half : K * (half + 1)].rearrange("h q m -> q h m")
+                src = t["y_plane", half][32 * q : 32 * q + 4, :].rearrange("q (h m) -> q h m", h=2)
+                queue.dma_start(out=dst.bitcast(I32), in_=src.bitcast(I32))
+
+        def constants():
+            make_identity(nc, ident[:])
+            nc.vector.memset(z_plane[:].bitcast(I32), 0)
+            nc.vector.memset(b_plane[:].bitcast(I32), 0)
+            nc.vector.memset(warm[:], 0.0)
+            nc.scalar.activation(out=warm[:, 4:5], in_=warm[:, 0:1], func=ACT.Identity)
+
+        def small_loads(queue):
+            queue.dma_start(out=rho_bf[:].rearrange("p (g j) -> p g j", j=4), in_=rho.rearrange("(g p j) -> p g j", p=P, j=4))
+            queue.dma_start(out=rhs_bf[:].rearrange("p (g j) -> p g j", j=4), in_=b.rearrange("(g p j) -> p g j", p=P, j=4))
+
+        def small_prep():
+            nc.vector.tensor_copy(out=rho_f[:], in_=rho_bf[:])
+            nc.vector.scalar_tensor_tensor(
+                out=shift[:], in0=rhs_bf[:], scalar=-1.0, in1=rho_bf[:], op0=ALU.mult, op1=ALU.mult
+            )
+
+        def load_z(half):
+            t["z", half] = kept("z_codes%d" % half, [P, K], U32)
+            src = z_words[0, :, K * half : K * (half + 1), :].rearrange("p n t -> p (n t)")
+            nc.sync.dma_start(out=t["z", half][:].bitcast(I32), in_=src.bitcast(I32))
+
+        def load_b():
+            nc.sync.dma_start(out=b_codes[:].bitcast(I32), in_=B_words[0].bitcast(I32))
+
+        def load_d():
+            nc.sync.dma_start(out=d_row[:], in_=d.partition_broadcast(P))
+
+        constants()
+        load_plane(nc.sync, z_plane, z_scales, range(3))
+        load_z(0)
+        load_b()
+        load_x0(0)
+        load_plane(nc.sync, z_plane, z_scales, [3])
+        load_plane(nc.sync, b_plane, B_scales, range(4))
+        load_x0(1)
+        load_a(0, 0)
+        load_x0(2)
+        load_a(0, 1)
+        load_x0(3)
+        small_loads(nc.sync)
+        load_a(1, 0)
+        load_lam(0)
+        load_a(1, 1)
+        load_lam(2)
+        load_z(1)
+        load_x0(4)
+        load_a_whole(2)
+        load_lam(1)
+        load_lam(3)
+        load_a_whole(3)
+        load_d()
+
+        for i in range(3):
+            s1_mm(i, 0)
+            s1_mm(i, 1)
+            w_add(i, 0)
+            w_add(i, 1)
+        for i in range(2):
+            w_turn(i)
+            w_copy(i)
+            at_turn(0, i)
+            at_copy(0, i)
+        s1_mm(3, 0)
+        s1_mm(3, 1)
+        small_prep()
+        at_quant(0, 0)
+        w_add(3, 0)
+        w_quant(0)
+        w_add(3, 1)
+        at_quant(0, 1)
+        load_x0(5)
+        load_x0(6)
+        at_turn(0, 2)
+        at_turn(0, 3)
+        w_turn(2)
+        at_copy(0, 2)
+        at_copy(0, 3)
+        w_copy(2)
+        a_weave(0, True)
+
+        UNITS = [4 * ch + g for g in range(4) for ch in range(2)] + list(range(8, 16))
+        LAM = [4, 5, 6, 7]
+        WEAVE = {-1: [(0, True)], 0: [(1, True)], 1: [(2, False)], 2: [(3, False)], 3: [(4, False)], 4: [(5, False)], 5: [(6, False), (8, True)], 6: [(7, False)], 7: [(9, False), (10, False)], 8: [(11, False)], 9: [(12, False), (13, True)], 10: [(14, False), (15, True)]}
+        S3 = {8: [(0, 0)], 9: [(1, 0)], 10: [(2, 0)], 11: [(3, 0)], 12: [(0, 1), (1, 1)], 13: [(2, 1), (3, 1)], 14: [(4, 0), (5, 0)], 15: [(4, 1), (5, 1)]}
+        AT = {-1: [(0, 2), (0, 3)], 0: [(1, 0), (1, 1)], 1: [(1, 2), (1, 3)], 2: [(2, 0), (2, 1)], 3: [(2, 2), (2, 3)], 4: [(3, 0), (3, 1)], 5: [(3, 2), (3, 3)]}
+        S1 = {1: [(4, 0)], 2: [(4, 1)], 3: [(5, 0)], 4: [(5, 1)], 7: [(6, 0)], 8: [(6, 1)], 9: [(7, 0), (7, 1)]}
+        WT = {3: 4, 5: 5, 9: 6, 10: 7}
+        WQ = {0: 1, 6: 2, 11: 3}
+        to_round, to_turn, to_quant = [], [], []
+        for n in range(16):
+            for g, j in AT.get(n - 1, []):
+                at_quant(g, j)
+            s2_mm(UNITS[n], 0)
+            violation(UNITS[n], 0)
+            if n == 0:
+                s2_mm(UNITS[n], 1)
+                w_turn(3)
+                w_copy(3)
+                violation(UNITS[n], 1)
+            for g, j in AT.get(n, []):
+                at_turn(g, j)
+            for tile, hh in S1.get(n, []):
+                s1_mm(tile, hh)
+            if n > 0:
+                s2_mm(UNITS[n], 1)
+            for g, j in AT.get(n, []):
+                at_copy(g, j)
+            if n > 0:
+                violation(UNITS[n], 1)
+            if n == 15:
+                lam_turn(UNITS[n])
+            for piece, on_v in WEAVE.get(n - 2, []):
+                a_quant(piece)
+            if n >= 1:
+                mu_add(UNITS[n - 1])
+            if n >= 2:
+                mu_quant(UNITS[n - 2])
+            for i, h in S3.get(n, []):
+                s3_mm(i, h, range(4))
+            for i, h in to_round:
+                y_round(i, h)
+                if i % 2 == 1:
+                    to_turn.append((i // 2, h))
+            to_round = []
+            for tile, hh in S1.get(n, []):
+                w_add(tile, hh)
+                if hh == 1 and tile + 3 < 8:
+                    load_x0(tile + 3)
+            for pair, h in to_quant:
+                y_quant(pair, h)
+                if h == 1:
+                    codes_store(pair)
+                if (pair, h) == (1, 1):
+                    plane_store(0, nc.sync)
+            to_quant = []
+            if n >= 1:
+                mu_cut(UNITS[n - 1])
+            if n in WQ:
+                w_quant(WQ[n])
+            for piece, on_v in WEAVE.get(n, []):
+                a_weave(piece, on_v)
+            if n < 15:
+                for i, h in S3.get(n, []):
+                    y_scale(i, h)
+                    to_round.append((i, h))
+                    if i % 2 == 1:
+                        y_store(i // 2, h)
+                lam_turn(UNITS[n])
+            if n in (2, 3, 6, 7):
+                load_lam(LAM.pop(0))
+            if n > 0 and n in WT:
+                w_turn(WT[n])
+                w_copy(WT[n])
+            for pair, h in to_turn:
+                y_turn(2 * pair, h)
+                y_turn(2 * pair + 1, h)
+                y_copy(pair, h)
+                to_quant.append((pair, h))
+            to_turn = []
+
+        mu_add(15)
+        mu_quant(14)
+        mu_cut(15)
+        y_scale(4, 1)
+        mu_quant(15)
+        y_scale(5, 1)
+        y_store(2, 1)
+        y_round(4, 1)
+        y_round(5, 1)
+        for pair, h in to_quant:
+            y_quant(pair, h)
+        for i, h in [(6, 0), (7, 0), (6, 1)]:
+            s3_mm(i, h, range(4))
+            y_scale(i, h)
+            y_round(i, h)
+            if (i, h) == (7, 0):
+                y_store(3, 0)
+                y_turn(4, 1)
+                y_turn(5, 1)
+                y_copy(2, 1)
+        y_quant(2, 1)
+        codes_store(2)
+        s3_mm(7, 1, range(4))
+        y_turn(6, 0)
+        y_turn(7, 0)
+        y_turn(6, 1)
+        y_copy(3, 0)
+        y_scale_round(7, 1)
+        y_scale(7, 1)
+        y_store(3, 1)
+        y_turn(7, 1)
+        y_copy(3, 1)
+        for h in range(2):
+            y_quant(3, h)
+        codes_store(3)
+        plane_store(1, nc.scalar)

@@ -114,12 +114,14 @@ def tile_augmented_lagrangian_inequality_grad_k1_kernel(
 
         def a_weave(piece, on_vector):
             h, g, part = piece // 8, piece % 8 // 2, piece % 2
-            t["a_bf", piece] = ringed("a_bf", [P, 1024], BF16, 4)
+            t["a_bf", piece] = ringed("a_bf_g", [P, 1024], BF16, 1) if on_vector == "G" else ringed("a_bf", [P, 1024], BF16, 4)
             first = K * h + 256 * part
             src = t["a", g][:].rearrange("p (j n) -> p j n", j=4)[:, :, first : first + 256]
             src = src.rearrange("p j (c i) -> p c j i", i=4)
             dst = t["a_bf", piece][:].rearrange("p (c i j) -> p c j i", i=4, j=4)
-            if on_vector:
+            if on_vector == "G":
+                nc.gpsimd.tensor_scalar(out=dst, in0=src, scalar1=1.0, scalar2=0.0, op0=ALU.mult, op1=ALU.add)
+            elif on_vector:
                 nc.vector.tensor_copy(out=dst, in_=src)
             else:
                 nc.scalar.copy(out=dst, in_=src)
@@ -208,7 +210,7 @@ def tile_augmented_lagrangian_inequality_grad_k1_kernel(
 
         def lam_turn(unit):
             words = t["lam", unit // 2][:].bitcast(F32)
-            tag = "lam_bank%d" % (unit % 2)
+            tag = "lam_bank%d" % (UNITS.index(unit) % 2)
             bank = t["lam_bank", unit] = psum.tile([P, K], F32, name=tag, tag=tag)
             for u in range(2):
                 for i in range(2):
@@ -218,16 +220,21 @@ def tile_augmented_lagrangian_inequality_grad_k1_kernel(
                     )
 
         def mu_add(unit):
-            t["mu", unit] = ringed("mu", [P, 1024], BF16, 3)
+            t["mu_sum", unit] = ringed("mu_sum", [P, 1024], BF16, 2)
             nc.vector.tensor_tensor(
-                out=t["mu", unit][:].rearrange("p (r u e) -> p r u e", u=2, e=2),
-                in0=t["lam_bank", unit][:].bitcast(BF16).rearrange("p (u r e) -> p r u e", u=2, e=2),
-                in1=t["viol", unit][:].rearrange("p (u e) r -> p r u e", u=2),
+                out=t["mu_sum", unit][:].rearrange("p (u r e) -> p u r e", u=2, e=2),
+                in0=t["lam_bank", unit][:].bitcast(BF16).rearrange("p (u r e) -> p u r e", u=2, e=2),
+                in1=t["viol", unit][:].rearrange("p (u e) r -> p u r e", u=2),
                 op=ALU.add,
             )
 
         def mu_cut(unit):
-            nc.vector.tensor_scalar_max(out=t["mu", unit][:], in0=t["mu", unit][:], scalar1=0.0)
+            t["mu", unit] = ringed("mu", [P, 1024], BF16, 2)
+            nc.vector.tensor_scalar_max(
+                out=t["mu", unit][:].rearrange("p (r u e) -> p r u e", u=2, e=2),
+                in0=t["mu_sum", unit][:].rearrange("p (u r e) -> p r u e", u=2, e=2),
+                scalar1=0.0,
+            )
 
         def mu_quant(unit):
             t["mu_codes", unit] = kept("mu_codes%d" % unit, [P, 256], U32)
@@ -318,9 +325,9 @@ def tile_augmented_lagrangian_inequality_grad_k1_kernel(
                 queue.dma_start(out=dst.bitcast(I32), in_=src.bitcast(I32))
 
         def constants():
+            nc.gpsimd.memset(z_plane[:].bitcast(I32), 0)
+            nc.gpsimd.memset(b_plane[:].bitcast(I32), 0)
             make_identity(nc, ident[:])
-            nc.vector.memset(z_plane[:].bitcast(I32), 0)
-            nc.vector.memset(b_plane[:].bitcast(I32), 0)
             nc.vector.memset(warm[:], 0.0)
             nc.scalar.activation(out=warm[:, 4:5], in_=warm[:, 0:1], func=ACT.Identity)
 
@@ -398,18 +405,35 @@ def tile_augmented_lagrangian_inequality_grad_k1_kernel(
         w_copy(2)
         a_weave(0, True)
 
+
         UNITS = [4 * ch + g for g in range(4) for ch in range(2)] + list(range(8, 16))
         LAM = [4, 5, 6, 7]
         WEAVE = {-1: [(0, True)], 0: [(1, True)], 1: [(2, False)], 2: [(3, False)], 3: [(4, False)], 4: [(5, False)], 5: [(6, False), (8, True)], 6: [(7, False)], 7: [(9, False), (10, False)], 8: [(11, False)], 9: [(12, False), (13, True)], 10: [(14, False), (15, True)]}
         S3 = {8: [(0, 0)], 9: [(1, 0)], 10: [(2, 0)], 11: [(3, 0)], 12: [(0, 1), (1, 1)], 13: [(2, 1), (3, 1)], 14: [(4, 0), (5, 0)], 15: [(4, 1), (5, 1)]}
         AT = {-1: [(0, 2), (0, 3)], 0: [(1, 0), (1, 1)], 1: [(1, 2), (1, 3)], 2: [(2, 0), (2, 1)], 3: [(2, 2), (2, 3)], 4: [(3, 0), (3, 1)], 5: [(3, 2), (3, 3)]}
-        S1 = {1: [(4, 0)], 2: [(4, 1)], 3: [(5, 0)], 4: [(5, 1)], 7: [(6, 0)], 8: [(6, 1)], 9: [(7, 0), (7, 1)]}
-        WT = {3: 4, 5: 5, 9: 6, 10: 7}
-        WQ = {0: 1, 6: 2, 11: 3}
+        S1 = {1: [(4, 0)], 2: [(4, 1)], 3: [(5, 0)], 4: [(5, 1)], 6: [(6, 0)], 7: [(6, 1)], 8: [(7, 0)], 9: [(7, 1)]}
+        WT = {3: 4, 5: 5, 8: 6, 9: 7}
+        WQ = {0: 1, 6: 2, 10: 3}
         to_round, to_turn, to_quant = [], [], []
         for n in range(16):
             for g, j in AT.get(n - 1, []):
                 at_quant(g, j)
+            for piece, eng in WEAVE.get(n - 2, []):
+                if eng != "G":
+                    a_quant(piece)
+            for piece, eng in WEAVE.get(n - 1, []):
+                if eng == "G":
+                    a_quant(piece)
+            for piece, eng in WEAVE.get(n, []):
+                if eng == "G":
+                    a_weave(piece, eng)
+            for i, h in S3.get(n - 1, []):
+                y_scale(i, h)
+                to_round.append((i, h))
+                if i % 2 == 1:
+                    y_store(i // 2, h)
+            for tile, hh in S1.get(n, []):
+                s1_mm(tile, hh)
             s2_mm(UNITS[n], 0)
             violation(UNITS[n], 0)
             if n == 0:
@@ -419,8 +443,6 @@ def tile_augmented_lagrangian_inequality_grad_k1_kernel(
                 violation(UNITS[n], 1)
             for g, j in AT.get(n, []):
                 at_turn(g, j)
-            for tile, hh in S1.get(n, []):
-                s1_mm(tile, hh)
             if n > 0:
                 s2_mm(UNITS[n], 1)
             for g, j in AT.get(n, []):
@@ -429,10 +451,12 @@ def tile_augmented_lagrangian_inequality_grad_k1_kernel(
                 violation(UNITS[n], 1)
             if n == 15:
                 lam_turn(UNITS[n])
-            for piece, on_v in WEAVE.get(n - 2, []):
-                a_quant(piece)
             if n >= 1:
                 mu_add(UNITS[n - 1])
+            for tile, hh in S1.get(n, []):
+                w_add(tile, hh)
+                if hh == 1 and tile + 3 < 8:
+                    load_x0(tile + 3)
             if n >= 2:
                 mu_quant(UNITS[n - 2])
             for i, h in S3.get(n, []):
@@ -442,10 +466,6 @@ def tile_augmented_lagrangian_inequality_grad_k1_kernel(
                 if i % 2 == 1:
                     to_turn.append((i // 2, h))
             to_round = []
-            for tile, hh in S1.get(n, []):
-                w_add(tile, hh)
-                if hh == 1 and tile + 3 < 8:
-                    load_x0(tile + 3)
             for pair, h in to_quant:
                 y_quant(pair, h)
                 if h == 1:
@@ -457,14 +477,10 @@ def tile_augmented_lagrangian_inequality_grad_k1_kernel(
                 mu_cut(UNITS[n - 1])
             if n in WQ:
                 w_quant(WQ[n])
-            for piece, on_v in WEAVE.get(n, []):
-                a_weave(piece, on_v)
+            for piece, eng in WEAVE.get(n, []):
+                if eng != "G":
+                    a_weave(piece, eng)
             if n < 15:
-                for i, h in S3.get(n, []):
-                    y_scale(i, h)
-                    to_round.append((i, h))
-                    if i % 2 == 1:
-                        y_store(i // 2, h)
                 lam_turn(UNITS[n])
             if n in (2, 3, 6, 7):
                 load_lam(LAM.pop(0))

@@ -112,16 +112,22 @@ def tile_augmented_lagrangian_inequality_grad_k1_kernel(
                 in_=t["at_bf", g, j][:].bitcast(BF16),
             )
 
-        def a_weave(piece, on_vector):
+        def a_weave(piece, eng, lo=0, hi=256):
             h, g, part = piece // 8, piece % 8 // 2, piece % 2
-            t["a_bf", piece] = ringed("a_bf_g", [P, 1024], BF16, 1) if on_vector == "G" else ringed("a_bf", [P, 1024], BF16, 4)
+            if lo == 0:
+                t["a_bf", piece] = ringed("a_bf_g", [P, 1024], BF16, 1) if eng in ("G", "VG") else ringed("a_bf", [P, 1024], BF16, 3)
             first = K * h + 256 * part
-            src = t["a", g][:].rearrange("p (j n) -> p j n", j=4)[:, :, first : first + 256]
+            src = t["a", g][:].rearrange("p (j n) -> p j n", j=4)[:, :, first + lo : first + hi]
+            dst = t["a_bf", piece][:, 4 * lo : 4 * hi]
+            if eng == "G":
+                nc.gpsimd.tensor_scalar(
+                    out=dst.rearrange("p (n j) -> p n j", j=4), in0=src.rearrange("p j n -> p n j"),
+                    scalar1=1.0, scalar2=0.0, op0=ALU.mult, op1=ALU.add,
+                )
+                return
             src = src.rearrange("p j (c i) -> p c j i", i=4)
-            dst = t["a_bf", piece][:].rearrange("p (c i j) -> p c j i", i=4, j=4)
-            if on_vector == "G":
-                nc.gpsimd.tensor_scalar(out=dst, in0=src, scalar1=1.0, scalar2=0.0, op0=ALU.mult, op1=ALU.add)
-            elif on_vector:
+            dst = dst.rearrange("p (c i j) -> p c j i", i=4, j=4)
+            if eng:
                 nc.vector.tensor_copy(out=dst, in_=src)
             else:
                 nc.scalar.copy(out=dst, in_=src)
@@ -208,16 +214,25 @@ def tile_augmented_lagrangian_inequality_grad_k1_kernel(
                     scale=rho_f[:, 4 * g + j : 4 * g + j + 1],
                 )
 
+        def lam_sort(unit):
+            words = t["lam", unit // 2][:].bitcast(F32).rearrange("r (i g p u) -> r g u i p", i=2, g=2, u=2)
+            t["lam_sorted", unit] = ringed("lam_sorted", [P, K], F32, 3)
+            nc.scalar.copy(
+                out=t["lam_sorted", unit][:].rearrange("r (u i p) -> r u i p", u=2, i=2), in_=words[:, unit % 2]
+            )
+
         def lam_turn(unit):
-            words = t["lam", unit // 2][:].bitcast(F32)
             tag = "lam_bank%d" % (UNITS.index(unit) % 2)
             bank = t["lam_bank", unit] = psum.tile([P, K], F32, name=tag, tag=tag)
             for u in range(2):
                 for i in range(2):
-                    first = 512 * i + 256 * (unit % 2)
-                    nc.tensor.transpose(
-                        bank[:, P * (2 * u + i) : P * (2 * u + i + 1)], words[:, first + u : first + 256 : 2], ident[:]
-                    )
+                    cols = slice(P * (2 * u + i), P * (2 * u + i + 1))
+                    if ("lam_sorted", unit) in t:
+                        src = t["lam_sorted", unit][:, cols]
+                    else:
+                        first = 512 * i + 256 * (unit % 2)
+                        src = t["lam", unit // 2][:].bitcast(F32)[:, first + u : first + 256 : 2]
+                    nc.tensor.transpose(bank[:, cols], src, ident[:])
 
         def mu_add(unit):
             t["mu_sum", unit] = ringed("mu_sum", [P, 1024], BF16, 2)
@@ -271,14 +286,14 @@ def tile_augmented_lagrangian_inequality_grad_k1_kernel(
             nc.sync.dma_start(out=dst, in_=t["y", pair, h][:])
 
         def y_round(i, h):
-            t["y_rows", i, h] = ringed("y_rows", [P, K], BF16, 4)
+            t["y_rows", i, h] = ringed("y_rows", [P, K], BF16, 6)
             nc.scalar.copy(
                 out=t["y_rows", i, h][:].rearrange("r (u p e) -> r u p e", u=2, e=2),
                 in_=t["y", i // 2, h][:, i % 2, :].rearrange("r (p u e) -> r u p e", u=2, e=2),
             )
 
         def y_scale_round(i, h):
-            t["y_rows", i, h] = ringed("y_rows", [P, K], BF16, 4)
+            t["y_rows", i, h] = ringed("y_rows", [P, K], BF16, 6)
             nc.vector.tensor_tensor(
                 out=t["y_rows", i, h][:].rearrange("r (u p e) -> r u p e", u=2, e=2),
                 in0=t["s3", i, h][:].rearrange("r (p u e) -> r u p e", u=2, e=2),
@@ -294,23 +309,31 @@ def tile_augmented_lagrangian_inequality_grad_k1_kernel(
                 first = P * (2 * u + i % 2)
                 nc.tensor.transpose(t["y_bank", i // 2, h][:, first : first + P], words[:, P * u : P * (u + 1)], ident[:])
 
-        def y_copy(pair, h):
-            t["y_turned", pair, h] = ringed("y_turned", [P, K], F32, 2)
+        def y_copy(pair, h, lo=0, hi=2):
+            if lo == 0:
+                t["y_turned", pair, h] = ringed("y_turned", [P, K], F32, 3)
             nc.scalar.copy(
-                out=t["y_turned", pair, h][:].rearrange("p (r u) -> p r u", u=2),
-                in_=t["y_bank", pair, h][:].rearrange("p (u r) -> p r u", u=2),
+                out=t["y_turned", pair, h][:].rearrange("p (r u) -> p r u", u=2)[:, P * lo : P * hi],
+                in_=t["y_bank", pair, h][:].rearrange("p (u r) -> p r u", u=2)[:, P * lo : P * hi],
             )
 
-        def y_quant(pair, h):
+        def y_store_tile(i, h):
+            nc.sync.dma_start(out=out_0[P * i : P * (i + 1), K * h : K * (h + 1)], in_=t["y", i // 2, h][:, i % 2, :])
+
+        def codes_store_half(pair, h):
+            dst = out_1[h, :, 256 * pair : 256 * (pair + 1), :].rearrange("p m t -> p (m t)")
+            nc.sync.dma_start(out=dst.bitcast(I32), in_=t["y_codes", pair][:, 256 * h : 256 * (h + 1)].bitcast(I32))
+
+        def y_quant(pair, h, lo=0, hi=2):
             if ("y_codes", pair) not in t:
                 t["y_codes", pair] = kept("y_codes%d" % pair, [P, K], U32)
             if ("y_plane", pair // 2) not in t:
                 t["y_plane", pair // 2] = kept("y_plane%d" % (pair // 2), [P, 2 * K], U8)
             first = K * h + 256 * (pair % 2)
             nc.vector.quantize_mx(
-                out=t["y_codes", pair][:, 256 * h : 256 * (h + 1)].bitcast(FP8X4),
-                scales=t["y_plane", pair // 2][:, first : first + 256],
-                in_=t["y_turned", pair, h][:].bitcast(BF16),
+                out=t["y_codes", pair][:, 256 * h + P * lo : 256 * h + P * hi].bitcast(FP8X4),
+                scales=t["y_plane", pair // 2][:, first + P * lo : first + P * hi],
+                in_=t["y_turned", pair, h][:, 256 * lo : 256 * hi].bitcast(BF16),
             )
 
         def codes_store(pair):
@@ -368,61 +391,64 @@ def tile_augmented_lagrangian_inequality_grad_k1_kernel(
         load_a(1, 0)
         load_lam(0)
         load_a(1, 1)
-        load_lam(2)
         load_z(1)
         load_x0(4)
+        load_lam(2)
         load_a_whole(2)
         load_lam(1)
         load_lam(3)
         load_a_whole(3)
         load_d()
 
-        for i in range(3):
+        for i in range(2):
             s1_mm(i, 0)
             s1_mm(i, 1)
             w_add(i, 0)
             w_add(i, 1)
+        small_prep()
         for i in range(2):
             w_turn(i)
             w_copy(i)
             at_turn(0, i)
             at_copy(0, i)
-        s1_mm(3, 0)
-        s1_mm(3, 1)
-        small_prep()
-        at_quant(0, 0)
-        w_add(3, 0)
-        w_quant(0)
-        w_add(3, 1)
-        at_quant(0, 1)
+            s1_mm(i + 2, 0)
+            s1_mm(i + 2, 1)
+            if i == 1:
+                w_quant(0)
+                at_quant(0, 1)
+            w_add(i + 2, 0)
+            w_add(i + 2, 1)
+            if i == 0:
+                at_quant(0, 0)
         load_x0(5)
         load_x0(6)
         at_turn(0, 2)
         at_turn(0, 3)
-        w_turn(2)
         at_copy(0, 2)
         at_copy(0, 3)
-        w_copy(2)
         a_weave(0, True)
 
 
         UNITS = [4 * ch + g for g in range(4) for ch in range(2)] + list(range(8, 16))
         LAM = [4, 5, 6, 7]
-        WEAVE = {-1: [(0, True)], 0: [(1, True)], 1: [(2, False)], 2: [(3, False)], 3: [(4, False)], 4: [(5, False)], 5: [(6, False), (8, True)], 6: [(7, False)], 7: [(9, False), (10, False)], 8: [(11, False)], 9: [(12, False), (13, True)], 10: [(14, False), (15, True)]}
+        WEAVE = {0: [(1, "VG")], 1: [(2, "G")], 2: [(3, "G")], 3: [(4, "G")], 4: [(5, "G")], 5: [(6, "G"), (8, False)], 6: [(7, "G"), (9, False)], 7: [(12, "G"), (10, False)], 8: [(13, "G"), (11, False)], 9: [(14, "G")], 10: [(15, "G")], -1: [(0, True)]}
         S3 = {8: [(0, 0)], 9: [(1, 0)], 10: [(2, 0)], 11: [(3, 0)], 12: [(0, 1), (1, 1)], 13: [(2, 1), (3, 1)], 14: [(4, 0), (5, 0)], 15: [(4, 1), (5, 1)]}
-        AT = {-1: [(0, 2), (0, 3)], 0: [(1, 0), (1, 1)], 1: [(1, 2), (1, 3)], 2: [(2, 0), (2, 1)], 3: [(2, 2), (2, 3)], 4: [(3, 0), (3, 1)], 5: [(3, 2), (3, 3)]}
-        S1 = {1: [(4, 0)], 2: [(4, 1)], 3: [(5, 0)], 4: [(5, 1)], 6: [(6, 0)], 7: [(6, 1)], 8: [(7, 0)], 9: [(7, 1)]}
-        WT = {3: 4, 5: 5, 8: 6, 9: 7}
+        AT = {-1: [(0, 2), (0, 3)], 1: [(1, 1), (1, 2)], 2: [(2, 0), (2, 1)], 3: [(2, 2), (2, 3)], 4: [(3, 0), (3, 1)], 5: [(3, 2), (3, 3)]}
+        AT_LATE = {0: [(1, 0)], 1: [(1, 3)]}
+        S1 = {n: [(4 + (n - 1) // 2, (n - 1) % 2)] for n in range(1, 9)}
+        WT = {3: 4, 5: 5, 7: 6, 9: 7}
         WQ = {0: 1, 6: 2, 10: 3}
         to_round, to_turn, to_quant = [], [], []
         for n in range(16):
-            for g, j in AT.get(n - 1, []):
+            for g, j in AT.get(n - 1, []) + AT_LATE.get(n - 1, []):
                 at_quant(g, j)
             for piece, eng in WEAVE.get(n - 2, []):
-                if eng != "G":
+                if eng not in ("G", "VG"):
                     a_quant(piece)
+            if n >= 2:
+                mu_quant(UNITS[n - 2])
             for piece, eng in WEAVE.get(n - 1, []):
-                if eng == "G":
+                if eng in ("G", "VG"):
                     a_quant(piece)
             for piece, eng in WEAVE.get(n, []):
                 if eng == "G":
@@ -437,9 +463,10 @@ def tile_augmented_lagrangian_inequality_grad_k1_kernel(
             s2_mm(UNITS[n], 0)
             violation(UNITS[n], 0)
             if n == 0:
+                for i in (2, 3):
+                    w_turn(i)
+                    w_copy(i)
                 s2_mm(UNITS[n], 1)
-                w_turn(3)
-                w_copy(3)
                 violation(UNITS[n], 1)
             for g, j in AT.get(n, []):
                 at_turn(g, j)
@@ -451,14 +478,14 @@ def tile_augmented_lagrangian_inequality_grad_k1_kernel(
                 violation(UNITS[n], 1)
             if n == 15:
                 lam_turn(UNITS[n])
+            elif n + 1 >= 11:
+                lam_sort(UNITS[n + 1])
             if n >= 1:
                 mu_add(UNITS[n - 1])
             for tile, hh in S1.get(n, []):
                 w_add(tile, hh)
                 if hh == 1 and tile + 3 < 8:
                     load_x0(tile + 3)
-            if n >= 2:
-                mu_quant(UNITS[n - 2])
             for i, h in S3.get(n, []):
                 s3_mm(i, h, range(4))
             for i, h in to_round:
@@ -466,6 +493,10 @@ def tile_augmented_lagrangian_inequality_grad_k1_kernel(
                 if i % 2 == 1:
                     to_turn.append((i // 2, h))
             to_round = []
+            if n >= 1 and not S1.get(n):
+                pass
+            if n >= 1:
+                mu_cut(UNITS[n - 1])
             for pair, h in to_quant:
                 y_quant(pair, h)
                 if h == 1:
@@ -473,15 +504,16 @@ def tile_augmented_lagrangian_inequality_grad_k1_kernel(
                 if (pair, h) == (1, 1):
                     plane_store(0, nc.sync)
             to_quant = []
-            if n >= 1:
-                mu_cut(UNITS[n - 1])
-            if n in WQ:
-                w_quant(WQ[n])
             for piece, eng in WEAVE.get(n, []):
                 if eng != "G":
                     a_weave(piece, eng)
+            if n in WQ:
+                w_quant(WQ[n])
             if n < 15:
                 lam_turn(UNITS[n])
+            for g, j in AT_LATE.get(n, []):
+                at_turn(g, j)
+                at_copy(g, j)
             if n in (2, 3, 6, 7):
                 load_lam(LAM.pop(0))
             if n > 0 and n in WT:
@@ -494,12 +526,12 @@ def tile_augmented_lagrangian_inequality_grad_k1_kernel(
                 to_quant.append((pair, h))
             to_turn = []
 
-        mu_add(15)
         mu_quant(14)
-        mu_cut(15)
+        mu_add(15)
         y_scale(4, 1)
-        mu_quant(15)
+        mu_cut(15)
         y_scale(5, 1)
+        mu_quant(15)
         y_store(2, 1)
         y_round(4, 1)
         y_round(5, 1)
@@ -516,17 +548,18 @@ def tile_augmented_lagrangian_inequality_grad_k1_kernel(
                 y_copy(2, 1)
         y_quant(2, 1)
         codes_store(2)
+        y_store_tile(6, 1)
         s3_mm(7, 1, range(4))
-        y_turn(6, 0)
-        y_turn(7, 0)
-        y_turn(6, 1)
+        for i, h in [(6, 0), (7, 0), (6, 1)]:
+            y_turn(i, h)
         y_copy(3, 0)
         y_scale_round(7, 1)
         y_scale(7, 1)
-        y_store(3, 1)
+        y_store_tile(7, 1)
         y_turn(7, 1)
         y_copy(3, 1)
-        for h in range(2):
-            y_quant(3, h)
-        codes_store(3)
+        y_quant(3, 0)
+        codes_store_half(3, 0)
+        y_quant(3, 1)
+        codes_store_half(3, 1)
         plane_store(1, nc.scalar)

@@ -18,9 +18,18 @@ ACT = mybir.ActivationFunctionType
 
 P = 128
 K = 512
-N_PASSES = N // K
-C_PASSES = C // K
-BANKS = 6
+CHUNK = 2 * P
+HALVES = N // K
+GROUPS = C // K
+STEPS = (R // CHUNK) * GROUPS
+PIECE = 256
+ROTATING_BANKS = 6
+
+UNITS = [GROUPS * ch + g for g in range(GROUPS) for ch in range(2)] + list(range(2 * GROUPS, STEPS))
+
+GPSIMD_COLUMNS = 176
+FIRST_SORTED_STEP = 11
+FIRST_SCALAR_PIECE_STEP = 5
 
 
 def tile_augmented_lagrangian_inequality_grad_k1_kernel(
@@ -34,11 +43,11 @@ def tile_augmented_lagrangian_inequality_grad_k1_kernel(
         ctx.enter_context(tc.manual_schedule())
 
         t = {}
-        bank_count = [0]
+        banks_taken = [0]
 
         def next_bank():
-            tag = "bank%d" % (bank_count[0] % BANKS)
-            bank_count[0] = bank_count[0] + 1
+            tag = "bank%d" % (banks_taken[0] % ROTATING_BANKS)
+            banks_taken[0] = banks_taken[0] + 1
             return psum.tile([P, K], F32, name=tag, tag=tag)
 
         def kept(name, shape, dtype):
@@ -47,51 +56,59 @@ def tile_augmented_lagrangian_inequality_grad_k1_kernel(
         def ringed(name, shape, dtype, bufs):
             return ring.tile(shape, dtype, name=name, tag=name, bufs=bufs, align_bytes=64)
 
+        def quantize(codes, plane, values):
+            nc.vector.quantize_mx(out=codes.bitcast(FP8X4), scales=plane, in_=values)
+
         ident = kept("ident", [P, P], F32)
         z_plane = kept("z_plane", [P, R], U8)
         b_codes = kept("b_codes", [P, 2 * N], U8)
         b_plane = kept("b_plane", [P, N], U8)
-        rho_bf = kept("rho_bf", [P, 16], BF16)
-        rhs_bf = kept("rhs_bf", [P, 16], BF16)
-        rho_f = kept("rho_f", [P, 16], F32)
-        shift = kept("shift", [P, 16], F32)
+        rho_bf = kept("rho_bf", [P, 4 * GROUPS], BF16)
+        bound_bf = kept("bound_bf", [P, 4 * GROUPS], BF16)
+        rho_f = kept("rho_f", [P, 4 * GROUPS], F32)
+        shift = kept("shift", [P, 4 * GROUPS], F32)
         d_row = kept("d_row", [P, N], BF16)
         warm = kept("warm", [P, 8], F32)
 
-        def load_a(g, half):
-            if half == 0:
-                t["a", g] = kept("a_raw%d" % g, [P, 4 * N], BF16)
-            cols = slice(2 * N * half, 2 * N * (half + 1))
-            rows = A[K * g : K * (g + 1), :].rearrange("(p j) n -> p (j n)", j=4)
-            nc.sync.dma_start(out=t["a", g][:, cols], in_=rows[:, cols])
-
-        def load_a_whole(g):
-            t["a", g] = kept("a_raw%d" % g, [P, 4 * N], BF16)
-            rows = A[K * g : K * (g + 1), :].rearrange("(p j) n -> p (j n)", j=4)
-            nc.sync.dma_start(out=t["a", g][:], in_=rows)
-
-        def load_plane(queue, plane, rows, quadrants):
+        def load_plane(plane, rows, quadrants):
             for q in quadrants:
-                queue.dma_start(
+                nc.sync.dma_start(
                     out=plane[32 * q : 32 * q + 4, :].bitcast(I32), in_=rows[0, 4 * q : 4 * q + 4, :].bitcast(I32)
                 )
+
+        def load_z(half):
+            t["z", half] = kept("z_codes%d" % half, [P, K], U32)
+            src = z_words[0, :, K * half : K * (half + 1), :].rearrange("p n t -> p (n t)")
+            nc.sync.dma_start(out=t["z", half][:].bitcast(I32), in_=src.bitcast(I32))
+
+        def load_a(g, first_slot, slots):
+            if first_slot == 0:
+                t["a", g] = kept("a_raw%d" % g, [P, 4 * N], BF16)
+            cols = slice(N * first_slot, N * (first_slot + slots))
+            rows = A[K * g : K * (g + 1), :].rearrange("(p j) n -> p (j n)", j=4)
+            nc.sync.dma_start(out=t["a", g][:, cols], in_=rows[:, cols])
 
         def load_x0(i):
             t["x0", i] = ringed("x0", [P, N], BF16, 5)
             nc.sync.dma_start(out=t["x0", i][:], in_=x0[P * i : P * (i + 1), :])
 
-        def load_lam(step):
-            ch, half = divmod(step, 2)
-            t["lam", step] = ringed("lam", [P, 2 * 1024], BF16, 4)
-            rows = lam[2 * P * ch : 2 * P * (ch + 1), 1024 * half : 1024 * (half + 1)].rearrange("(i p) c -> p i c", p=P)
-            nc.sync.dma_start(out=t["lam", step][:].rearrange("p (i c) -> p i c", i=2), in_=rows)
+        def load_lam(unit):
+            ch, g = divmod(unit, GROUPS)
+            t["lam", unit // 2] = ringed("lam", [P, 4 * K], BF16, 4)
+            rows = lam[CHUNK * ch : CHUNK * (ch + 1), K * g : K * (g + 2)].rearrange("(i p) c -> p i c", p=P)
+            nc.sync.dma_start(out=t["lam", unit // 2][:].rearrange("p (i c) -> p i c", i=2), in_=rows)
+
+        def load_by_slot(tile, vector):
+            nc.sync.dma_start(
+                out=tile[:].rearrange("p (g j) -> p g j", j=4), in_=vector.rearrange("(g p j) -> p g j", p=P, j=4)
+            )
 
         def at_turn(g, j):
             words = t["a", g][:].bitcast(F32)
             bank = t["at_bank", g, j] = next_bank()
-            for h in range(N_PASSES):
+            for h in range(HALVES):
                 for u in range(2):
-                    first = 512 * j + 256 * h
+                    first = K * j + 256 * h
                     nc.tensor.transpose(
                         bank[:, P * (2 * h + u) : P * (2 * h + u + 1)], words[:, first + u : first + 256 : 2], ident[:]
                     )
@@ -104,43 +121,44 @@ def tile_augmented_lagrangian_inequality_grad_k1_kernel(
             )
 
         def at_quant(g, j):
-            t["at_codes", g, j] = kept("at_codes%d_%d" % (g, j), [P, 256], U32)
-            t["at_plane", g, j] = kept("at_plane%d_%d" % (g, j), [P, 256], U8)
-            nc.vector.quantize_mx(
-                out=t["at_codes", g, j][:].bitcast(FP8X4),
-                scales=t["at_plane", g, j][:],
-                in_=t["at_bf", g, j][:].bitcast(BF16),
+            t["at_codes", g, j] = kept("at_codes%d_%d" % (g, j), [P, HALVES * P], U32)
+            t["at_plane", g, j] = kept("at_plane%d_%d" % (g, j), [P, HALVES * P], U8)
+            quantize(t["at_codes", g, j][:], t["at_plane", g, j][:], t["at_bf", g, j][:].bitcast(BF16))
+
+        def piece_views(piece, lo, hi):
+            h, g, part = piece // 8, piece % 8 // 2, piece % 2
+            first = K * h + PIECE * part
+            src = t["a", g][:].rearrange("p (j n) -> p j n", j=4)[:, :, first + lo : first + hi]
+            return t["a_bf", piece][:, 4 * lo : 4 * hi], src
+
+        def weave(copy, piece, lo, hi):
+            dst, src = piece_views(piece, lo, hi)
+            copy(out=dst.rearrange("p (c i j) -> p c j i", i=4, j=4), in_=src.rearrange("p j (c i) -> p c j i", i=4))
+
+        def weave_gpsimd(piece):
+            dst, src = piece_views(piece, 0, GPSIMD_COLUMNS)
+            nc.gpsimd.tensor_scalar(
+                out=dst.rearrange("p (n j) -> p n j", j=4),
+                in0=src.rearrange("p j n -> p n j"),
+                scalar1=1.0,
+                scalar2=0.0,
+                op0=ALU.mult,
+                op1=ALU.add,
             )
 
-        def a_weave(piece, eng, lo=0, hi=256):
-            h, g, part = piece // 8, piece % 8 // 2, piece % 2
-            if lo == 0:
-                t["a_bf", piece] = ringed("a_bf_g", [P, 1024], BF16, 1) if eng in ("G", "VG") else ringed("a_bf", [P, 1024], BF16, 3)
-            first = K * h + 256 * part
-            src = t["a", g][:].rearrange("p (j n) -> p j n", j=4)[:, :, first + lo : first + hi]
-            dst = t["a_bf", piece][:, 4 * lo : 4 * hi]
-            if eng == "G":
-                nc.gpsimd.tensor_scalar(
-                    out=dst.rearrange("p (n j) -> p n j", j=4), in0=src.rearrange("p j n -> p n j"),
-                    scalar1=1.0, scalar2=0.0, op0=ALU.mult, op1=ALU.add,
-                )
-                return
-            src = src.rearrange("p j (c i) -> p c j i", i=4)
-            dst = dst.rearrange("p (c i j) -> p c j i", i=4, j=4)
-            if eng:
-                nc.vector.tensor_copy(out=dst, in_=src)
-            else:
-                nc.scalar.copy(out=dst, in_=src)
+        def own_piece(piece):
+            t["a_bf", piece] = ringed("a_bf", [P, 4 * PIECE], BF16, 3)
+
+        def shared_piece(piece):
+            t["a_bf", piece] = ringed("a_bf_shared", [P, 4 * PIECE], BF16, 1)
 
         def a_quant(piece):
             h, g, part = piece // 8, piece % 8 // 2, piece % 2
             if part == 0:
                 t["a_codes", g, h] = kept("a_codes%d_%d" % (g, h), [P, K], U32)
                 t["a_plane", g, h] = kept("a_plane%d_%d" % (g, h), [P, K], U8)
-            cols = slice(256 * part, 256 * (part + 1))
-            nc.vector.quantize_mx(
-                out=t["a_codes", g, h][:, cols].bitcast(FP8X4), scales=t["a_plane", g, h][:, cols], in_=t["a_bf", piece][:]
-            )
+            cols = slice(PIECE * part, PIECE * (part + 1))
+            quantize(t["a_codes", g, h][:, cols], t["a_plane", g, h][:, cols], t["a_bf", piece][:])
 
         def s1_mm(i, h):
             bank = t["s1", i, h] = next_bank()
@@ -166,49 +184,45 @@ def tile_augmented_lagrangian_inequality_grad_k1_kernel(
 
         def w_turn(i):
             words = t["w_rows", i][:].bitcast(F32)
-            bank = t["w_bank", i] = next_bank()
+            bank = next_bank()
             for q in range(4):
                 nc.tensor.transpose(bank[:, P * q : P * (q + 1)], words[:, P * q : P * (q + 1)], ident[:])
-
-        def w_copy(i):
             if i % 2 == 0:
-                t["w_turned", i // 2] = ringed("w_turned", [P, 1024], F32, 2)
+                t["w_turned", i // 2] = ringed("w_turned", [P, 2 * K], F32, 2)
             dst = t["w_turned", i // 2][:].rearrange("p (h i r u) -> p i h r u", h=2, i=2, u=2)
-            nc.scalar.copy(out=dst[:, i % 2], in_=t["w_bank", i][:].rearrange("p (h u r) -> p h r u", h=2, u=2))
+            nc.scalar.copy(out=dst[:, i % 2], in_=bank[:].rearrange("p (h u r) -> p h r u", h=2, u=2))
 
         def w_quant(ch):
-            t["w_codes", ch] = kept("w_codes%d" % ch, [P, K], U32)
-            t["w_plane", ch] = kept("w_plane%d" % ch, [P, K], U8)
-            nc.vector.quantize_mx(
-                out=t["w_codes", ch][:].bitcast(FP8X4), scales=t["w_plane", ch][:], in_=t["w_turned", ch][:].bitcast(BF16)
-            )
+            t["w_codes", ch] = kept("w_codes%d" % ch, [P, HALVES * CHUNK], U32)
+            t["w_plane", ch] = kept("w_plane%d" % ch, [P, HALVES * CHUNK], U8)
+            quantize(t["w_codes", ch][:], t["w_plane", ch][:], t["w_turned", ch][:].bitcast(BF16))
 
-        def s2_mm(unit, jj):
-            ch, g = divmod(unit, 4)
-            bank = t["s2", unit, jj] = next_bank()
+        def s2_mm(unit, u):
+            ch, g = divmod(unit, GROUPS)
+            bank = t["s2", unit, u] = next_bank()
             for e in range(2):
-                for h in range(N_PASSES):
+                for h in range(HALVES):
                     cols = slice(P * h, P * (h + 1))
-                    pts = slice(256 * h, 256 * (h + 1))
+                    points = slice(CHUNK * h, CHUNK * (h + 1))
                     nc.tensor.matmul_mx(
-                        out=bank[:, 256 * e : 256 * (e + 1)],
-                        lhsT=t["at_codes", g, 2 * jj + e][:, cols].bitcast(FP8X4),
-                        lhsT_scale=t["at_plane", g, 2 * jj + e][:, cols],
-                        rhs=t["w_codes", ch][:, pts].bitcast(FP8X4),
-                        rhs_scale=t["w_plane", ch][:, pts],
+                        out=bank[:, CHUNK * e : CHUNK * (e + 1)],
+                        lhsT=t["at_codes", g, 2 * u + e][:, cols].bitcast(FP8X4),
+                        lhsT_scale=t["at_plane", g, 2 * u + e][:, cols],
+                        rhs=t["w_codes", ch][:, points].bitcast(FP8X4),
+                        rhs_scale=t["w_plane", ch][:, points],
                         start=(h == 0),
-                        stop=(h == N_PASSES - 1),
+                        stop=(h == HALVES - 1),
                     )
 
-        def violation(unit, jj):
-            g = unit % 4
-            if jj == 0:
-                t["viol", unit] = ringed("viol", [P, 4, 256], F32, 3)
+        def violation(unit, u):
+            g = unit % GROUPS
+            if u == 0:
+                t["viol", unit] = ringed("viol", [P, 4, CHUNK], F32, 3)
             for e in range(2):
-                j = 2 * jj + e
+                j = 2 * u + e
                 nc.scalar.activation(
                     out=t["viol", unit][:, j, :],
-                    in_=t["s2", unit, jj][:, 256 * e : 256 * (e + 1)],
+                    in_=t["s2", unit, u][:, CHUNK * e : CHUNK * (e + 1)],
                     func=ACT.Identity,
                     bias=shift[:, 4 * g + j : 4 * g + j + 1],
                     scale=rho_f[:, 4 * g + j : 4 * g + j + 1],
@@ -221,21 +235,22 @@ def tile_augmented_lagrangian_inequality_grad_k1_kernel(
                 out=t["lam_sorted", unit][:].rearrange("r (u i p) -> r u i p", u=2, i=2), in_=words[:, unit % 2]
             )
 
-        def lam_turn(unit):
-            tag = "lam_bank%d" % (UNITS.index(unit) % 2)
+        def lam_turn(step):
+            unit = UNITS[step]
+            tag = "lam_bank%d" % (step % 2)
             bank = t["lam_bank", unit] = psum.tile([P, K], F32, name=tag, tag=tag)
             for u in range(2):
                 for i in range(2):
                     cols = slice(P * (2 * u + i), P * (2 * u + i + 1))
-                    if ("lam_sorted", unit) in t:
+                    if step >= FIRST_SORTED_STEP:
                         src = t["lam_sorted", unit][:, cols]
                     else:
-                        first = 512 * i + 256 * (unit % 2)
+                        first = K * i + 256 * (unit % 2)
                         src = t["lam", unit // 2][:].bitcast(F32)[:, first + u : first + 256 : 2]
                     nc.tensor.transpose(bank[:, cols], src, ident[:])
 
         def mu_add(unit):
-            t["mu_sum", unit] = ringed("mu_sum", [P, 1024], BF16, 2)
+            t["mu_sum", unit] = ringed("mu_sum", [P, 4 * CHUNK], BF16, 2)
             nc.vector.tensor_tensor(
                 out=t["mu_sum", unit][:].rearrange("p (u r e) -> p u r e", u=2, e=2),
                 in0=t["lam_bank", unit][:].bitcast(BF16).rearrange("p (u r e) -> p u r e", u=2, e=2),
@@ -244,7 +259,7 @@ def tile_augmented_lagrangian_inequality_grad_k1_kernel(
             )
 
         def mu_cut(unit):
-            t["mu", unit] = ringed("mu", [P, 1024], BF16, 2)
+            t["mu", unit] = ringed("mu", [P, 4 * CHUNK], BF16, 2)
             nc.vector.tensor_scalar_max(
                 out=t["mu", unit][:].rearrange("p (r u e) -> p r u e", u=2, e=2),
                 in0=t["mu_sum", unit][:].rearrange("p (u r e) -> p r u e", u=2, e=2),
@@ -252,26 +267,23 @@ def tile_augmented_lagrangian_inequality_grad_k1_kernel(
             )
 
         def mu_quant(unit):
-            t["mu_codes", unit] = kept("mu_codes%d" % unit, [P, 256], U32)
-            t["mu_plane", unit] = kept("mu_plane%d" % unit, [P, 256], U8)
-            nc.vector.quantize_mx(
-                out=t["mu_codes", unit][:].bitcast(FP8X4), scales=t["mu_plane", unit][:], in_=t["mu", unit][:]
-            )
+            t["mu_codes", unit] = kept("mu_codes%d" % unit, [P, CHUNK], U32)
+            t["mu_plane", unit] = kept("mu_plane%d" % unit, [P, CHUNK], U8)
+            quantize(t["mu_codes", unit][:], t["mu_plane", unit][:], t["mu", unit][:])
 
-        def s3_mm(i, h, passes):
+        def s3_mm(i, h):
             cols = slice(P * (i % 2), P * (i % 2 + 1))
-            for g in passes:
-                if g == 0:
-                    t["s3", i, h] = next_bank()
-                unit = 4 * (i // 2) + g
+            bank = t["s3", i, h] = next_bank()
+            for g in range(GROUPS):
+                unit = GROUPS * (i // 2) + g
                 nc.tensor.matmul_mx(
-                    out=t["s3", i, h][:],
+                    out=bank[:],
                     lhsT=t["mu_codes", unit][:, cols].bitcast(FP8X4),
                     lhsT_scale=t["mu_plane", unit][:, cols],
                     rhs=t["a_codes", g, h][:].bitcast(FP8X4),
                     rhs_scale=t["a_plane", g, h][:],
                     start=(g == 0),
-                    stop=(g == C_PASSES - 1),
+                    stop=(g == GROUPS - 1),
                 )
 
         def y_scale(i, h):
@@ -281,19 +293,22 @@ def tile_augmented_lagrangian_inequality_grad_k1_kernel(
                 out=t["y", i // 2, h][:, i % 2, :], in0=t["s3", i, h][:], in1=d_row[:, K * h : K * (h + 1)], op=ALU.mult
             )
 
-        def y_store(pair, h):
-            dst = out_0[2 * P * pair : 2 * P * (pair + 1), K * h : K * (h + 1)].rearrange("(i p) n -> p i n", p=P)
-            nc.sync.dma_start(out=dst, in_=t["y", pair, h][:])
+        def y_store(ch, h):
+            dst = out_0[CHUNK * ch : CHUNK * (ch + 1), K * h : K * (h + 1)].rearrange("(i p) n -> p i n", p=P)
+            nc.sync.dma_start(out=dst, in_=t["y", ch, h][:])
+
+        def y_store_tile(i, h):
+            nc.sync.dma_start(out=out_0[P * i : P * (i + 1), K * h : K * (h + 1)], in_=t["y", i // 2, h][:, i % 2, :])
 
         def y_round(i, h):
-            t["y_rows", i, h] = ringed("y_rows", [P, K], BF16, 6)
+            t["y_rows", i, h] = ringed("y_rows", [P, K], BF16, 7)
             nc.scalar.copy(
                 out=t["y_rows", i, h][:].rearrange("r (u p e) -> r u p e", u=2, e=2),
                 in_=t["y", i // 2, h][:, i % 2, :].rearrange("r (p u e) -> r u p e", u=2, e=2),
             )
 
         def y_scale_round(i, h):
-            t["y_rows", i, h] = ringed("y_rows", [P, K], BF16, 6)
+            t["y_rows", i, h] = ringed("y_rows", [P, K], BF16, 7)
             nc.vector.tensor_tensor(
                 out=t["y_rows", i, h][:].rearrange("r (u p e) -> r u p e", u=2, e=2),
                 in0=t["s3", i, h][:].rearrange("r (p u e) -> r u p e", u=2, e=2),
@@ -309,257 +324,252 @@ def tile_augmented_lagrangian_inequality_grad_k1_kernel(
                 first = P * (2 * u + i % 2)
                 nc.tensor.transpose(t["y_bank", i // 2, h][:, first : first + P], words[:, P * u : P * (u + 1)], ident[:])
 
-        def y_copy(pair, h, lo=0, hi=2):
-            if lo == 0:
-                t["y_turned", pair, h] = ringed("y_turned", [P, K], F32, 3)
+        def y_copy(ch, h):
+            t["y_turned", ch, h] = ringed("y_turned", [P, K], F32, 3)
             nc.scalar.copy(
-                out=t["y_turned", pair, h][:].rearrange("p (r u) -> p r u", u=2)[:, P * lo : P * hi],
-                in_=t["y_bank", pair, h][:].rearrange("p (u r) -> p r u", u=2)[:, P * lo : P * hi],
+                out=t["y_turned", ch, h][:].rearrange("p (r u) -> p r u", u=2),
+                in_=t["y_bank", ch, h][:].rearrange("p (u r) -> p r u", u=2),
             )
 
-        def y_store_tile(i, h):
-            nc.sync.dma_start(out=out_0[P * i : P * (i + 1), K * h : K * (h + 1)], in_=t["y", i // 2, h][:, i % 2, :])
+        def y_turn_chunk(ch, h):
+            y_turn(2 * ch, h)
+            y_turn(2 * ch + 1, h)
+            y_copy(ch, h)
 
-        def codes_store_half(pair, h):
-            dst = out_1[h, :, 256 * pair : 256 * (pair + 1), :].rearrange("p m t -> p (m t)")
-            nc.sync.dma_start(out=dst.bitcast(I32), in_=t["y_codes", pair][:, 256 * h : 256 * (h + 1)].bitcast(I32))
-
-        def y_quant(pair, h, lo=0, hi=2):
-            if ("y_codes", pair) not in t:
-                t["y_codes", pair] = kept("y_codes%d" % pair, [P, K], U32)
-            if ("y_plane", pair // 2) not in t:
-                t["y_plane", pair // 2] = kept("y_plane%d" % (pair // 2), [P, 2 * K], U8)
-            first = K * h + 256 * (pair % 2)
-            nc.vector.quantize_mx(
-                out=t["y_codes", pair][:, 256 * h + P * lo : 256 * h + P * hi].bitcast(FP8X4),
-                scales=t["y_plane", pair // 2][:, first + P * lo : first + P * hi],
-                in_=t["y_turned", pair, h][:, 256 * lo : 256 * hi].bitcast(BF16),
+        def y_quant(ch, h):
+            if h == 0:
+                t["y_codes", ch] = kept("y_codes%d" % ch, [P, HALVES * CHUNK], U32)
+                if ch % 2 == 0:
+                    t["y_plane", ch // 2] = kept("y_plane%d" % (ch // 2), [P, HALVES * 2 * CHUNK], U8)
+            first = 2 * CHUNK * h + CHUNK * (ch % 2)
+            quantize(
+                t["y_codes", ch][:, CHUNK * h : CHUNK * (h + 1)],
+                t["y_plane", ch // 2][:, first : first + CHUNK],
+                t["y_turned", ch, h][:].bitcast(BF16),
             )
 
-        def codes_store(pair):
-            dst = out_1[:, :, 256 * pair : 256 * (pair + 1), :].rearrange("h p m t -> p h (m t)")
-            src = t["y_codes", pair][:].rearrange("p (h m) -> p h m", h=2)
+        def codes_store(ch):
+            dst = out_1[:, :, CHUNK * ch : CHUNK * (ch + 1), :].rearrange("h p m t -> p h (m t)")
+            src = t["y_codes", ch][:].rearrange("p (h m) -> p h m", h=2)
             nc.sync.dma_start(out=dst.bitcast(I32), in_=src.bitcast(I32))
 
-        def plane_store(half, queue):
+        def codes_store_half(ch, h):
+            dst = out_1[h, :, CHUNK * ch : CHUNK * (ch + 1), :].rearrange("p m t -> p (m t)")
+            nc.sync.dma_start(out=dst.bitcast(I32), in_=t["y_codes", ch][:, CHUNK * h : CHUNK * (h + 1)].bitcast(I32))
+
+        def plane_store(pair, queue):
             for q in range(4):
-                dst = out_2[:, 4 * q : 4 * q + 4, K * half : K * (half + 1)].rearrange("h q m -> q h m")
-                src = t["y_plane", half][32 * q : 32 * q + 4, :].rearrange("q (h m) -> q h m", h=2)
+                dst = out_2[:, 4 * q : 4 * q + 4, 2 * CHUNK * pair : 2 * CHUNK * (pair + 1)].rearrange("h q m -> q h m")
+                src = t["y_plane", pair][32 * q : 32 * q + 4, :].rearrange("q (h m) -> q h m", h=2)
                 queue.dma_start(out=dst.bitcast(I32), in_=src.bitcast(I32))
 
-        def constants():
-            nc.gpsimd.memset(z_plane[:].bitcast(I32), 0)
-            nc.gpsimd.memset(b_plane[:].bitcast(I32), 0)
-            make_identity(nc, ident[:])
-            nc.vector.memset(warm[:], 0.0)
-            nc.scalar.activation(out=warm[:, 4:5], in_=warm[:, 0:1], func=ACT.Identity)
+        nc.gpsimd.memset(z_plane[:].bitcast(I32), 0)
+        nc.gpsimd.memset(b_plane[:].bitcast(I32), 0)
+        make_identity(nc, ident[:])
+        nc.vector.memset(warm[:], 0.0)
+        nc.scalar.activation(out=warm[:, 4:5], in_=warm[:, 0:1], func=ACT.Identity)
 
-        def small_loads(queue):
-            queue.dma_start(out=rho_bf[:].rearrange("p (g j) -> p g j", j=4), in_=rho.rearrange("(g p j) -> p g j", p=P, j=4))
-            queue.dma_start(out=rhs_bf[:].rearrange("p (g j) -> p g j", j=4), in_=b.rearrange("(g p j) -> p g j", p=P, j=4))
-
-        def small_prep():
-            nc.vector.tensor_copy(out=rho_f[:], in_=rho_bf[:])
-            nc.vector.scalar_tensor_tensor(
-                out=shift[:], in0=rhs_bf[:], scalar=-1.0, in1=rho_bf[:], op0=ALU.mult, op1=ALU.mult
-            )
-
-        def load_z(half):
-            t["z", half] = kept("z_codes%d" % half, [P, K], U32)
-            src = z_words[0, :, K * half : K * (half + 1), :].rearrange("p n t -> p (n t)")
-            nc.sync.dma_start(out=t["z", half][:].bitcast(I32), in_=src.bitcast(I32))
-
-        def load_b():
-            nc.sync.dma_start(out=b_codes[:].bitcast(I32), in_=B_words[0].bitcast(I32))
-
-        def load_d():
-            nc.sync.dma_start(out=d_row[:], in_=d.partition_broadcast(P))
-
-        constants()
-        load_plane(nc.sync, z_plane, z_scales, range(3))
+        load_plane(z_plane, z_scales, range(3))
         load_z(0)
-        load_b()
+        nc.sync.dma_start(out=b_codes[:].bitcast(I32), in_=B_words[0].bitcast(I32))
         load_x0(0)
-        load_plane(nc.sync, z_plane, z_scales, [3])
-        load_plane(nc.sync, b_plane, B_scales, range(4))
+        load_plane(z_plane, z_scales, [3])
+        load_plane(b_plane, B_scales, range(4))
         load_x0(1)
-        load_a(0, 0)
+        load_a(0, 0, 2)
         load_x0(2)
-        load_a(0, 1)
+        load_a(0, 2, 2)
         load_x0(3)
-        small_loads(nc.sync)
-        load_a(1, 0)
-        load_lam(0)
-        load_a(1, 1)
+        load_by_slot(rho_bf, rho)
+        load_by_slot(bound_bf, b)
+        load_a(1, 0, 2)
+        load_lam(UNITS[0])
+        load_a(1, 2, 2)
         load_z(1)
         load_x0(4)
-        load_lam(2)
-        load_a_whole(2)
-        load_lam(1)
-        load_lam(3)
-        load_a_whole(3)
-        load_d()
+        load_lam(UNITS[1])
+        load_a(2, 0, 4)
+        load_lam(UNITS[4])
+        load_lam(UNITS[5])
+        load_a(3, 0, 4)
+        nc.sync.dma_start(out=d_row[:], in_=d.partition_broadcast(P))
 
         for i in range(2):
-            s1_mm(i, 0)
-            s1_mm(i, 1)
-            w_add(i, 0)
-            w_add(i, 1)
-        small_prep()
-        for i in range(2):
+            for h in range(HALVES):
+                s1_mm(i, h)
+            for h in range(HALVES):
+                w_add(i, h)
+        nc.vector.tensor_copy(out=rho_f[:], in_=rho_bf[:])
+        nc.vector.scalar_tensor_tensor(
+            out=shift[:], in0=bound_bf[:], scalar=-1.0, in1=rho_bf[:], op0=ALU.mult, op1=ALU.mult
+        )
+
+        def turns_then_first_product(i):
             w_turn(i)
-            w_copy(i)
             at_turn(0, i)
             at_copy(0, i)
-            s1_mm(i + 2, 0)
-            s1_mm(i + 2, 1)
-            if i == 1:
-                w_quant(0)
-                at_quant(0, 1)
-            w_add(i + 2, 0)
-            w_add(i + 2, 1)
-            if i == 0:
-                at_quant(0, 0)
+            for h in range(HALVES):
+                s1_mm(i + 2, h)
+
+        turns_then_first_product(0)
+        for h in range(HALVES):
+            w_add(2, h)
+        at_quant(0, 0)
+        turns_then_first_product(1)
+        w_quant(0)
+        at_quant(0, 1)
+        for h in range(HALVES):
+            w_add(3, h)
         load_x0(5)
         load_x0(6)
-        at_turn(0, 2)
-        at_turn(0, 3)
-        at_copy(0, 2)
-        at_copy(0, 3)
-        a_weave(0, True)
+        turned = [(0, 2), (0, 3)]
+        for g, j in turned:
+            at_turn(g, j)
+        for g, j in turned:
+            at_copy(g, j)
+        own_piece(0)
+        weave(nc.vector.tensor_copy, 0, 0, PIECE)
 
+        slots_to_turn = [(g, j) for g in range(1, GROUPS) for j in range(4)]
+        first_products = [(i, h) for i in range(4, 8) for h in range(HALVES)]
+        shared_pieces = list(range(2, 8)) + list(range(12, 16))
+        scalar_pieces = list(range(8, 12))
+        lam_to_load = list(range(2 * GROUPS, STEPS, 2))
+        third_products = [(i, h) for h in range(HALVES) for i in range(4)]
+        third_products = third_products + [(i, h) for h in range(HALVES) for i in (4, 5)]
 
-        UNITS = [4 * ch + g for g in range(4) for ch in range(2)] + list(range(8, 16))
-        LAM = [4, 5, 6, 7]
-        WEAVE = {0: [(1, "VG")], 1: [(2, "G")], 2: [(3, "G")], 3: [(4, "G")], 4: [(5, "G")], 5: [(6, "G"), (8, False)], 6: [(7, "G"), (9, False)], 7: [(12, "G"), (10, False)], 8: [(13, "G"), (11, False)], 9: [(14, "G")], 10: [(15, "G")], -1: [(0, True)]}
-        S3 = {8: [(0, 0)], 9: [(1, 0)], 10: [(2, 0)], 11: [(3, 0)], 12: [(0, 1), (1, 1)], 13: [(2, 1), (3, 1)], 14: [(4, 0), (5, 0)], 15: [(4, 1), (5, 1)]}
-        AT = {-1: [(0, 2), (0, 3)], 1: [(1, 1), (1, 2)], 2: [(2, 0), (2, 1)], 3: [(2, 2), (2, 3)], 4: [(3, 0), (3, 1)], 5: [(3, 2), (3, 3)]}
-        AT_LATE = {0: [(1, 0)], 1: [(1, 3)]}
-        S1 = {n: [(4 + (n - 1) // 2, (n - 1) % 2)] for n in range(1, 9)}
-        WT = {3: 4, 5: 5, 7: 6, 9: 7}
-        WQ = {0: 1, 6: 2, 10: 3}
-        to_round, to_turn, to_quant = [], [], []
-        for n in range(16):
-            for g, j in AT.get(n - 1, []) + AT_LATE.get(n - 1, []):
+        def take(queue, count):
+            return [queue.pop(0) for k in range(min(count, len(queue)))]
+
+        own_woven = {-1: [0]}
+        shared_woven = []
+        multiplied, rounded, copied = [], [], []
+        for n in range(STEPS):
+            unit = UNITS[n]
+
+            for g, j in turned:
                 at_quant(g, j)
-            for piece, eng in WEAVE.get(n - 2, []):
-                if eng not in ("G", "VG"):
-                    a_quant(piece)
+            for piece in own_woven.get(n - 2, []):
+                a_quant(piece)
             if n >= 2:
                 mu_quant(UNITS[n - 2])
-            for piece, eng in WEAVE.get(n - 1, []):
-                if eng in ("G", "VG"):
-                    a_quant(piece)
-            for piece, eng in WEAVE.get(n, []):
-                if eng == "G":
-                    a_weave(piece, eng)
-            for i, h in S3.get(n - 1, []):
+            for piece in shared_woven:
+                a_quant(piece)
+            shared_woven = take(shared_pieces, 1 if n >= 1 else 0)
+            for piece in shared_woven:
+                shared_piece(piece)
+                weave_gpsimd(piece)
+
+            scaled, multiplied = multiplied, []
+            for i, h in scaled:
                 y_scale(i, h)
-                to_round.append((i, h))
                 if i % 2 == 1:
                     y_store(i // 2, h)
-            for tile, hh in S1.get(n, []):
-                s1_mm(tile, hh)
-            s2_mm(UNITS[n], 0)
-            violation(UNITS[n], 0)
+            summed = take(first_products, 1 if n >= 1 else 0)
+            for i, h in summed:
+                s1_mm(i, h)
+            s2_mm(unit, 0)
+            violation(unit, 0)
+            for piece in shared_woven:
+                weave(nc.scalar.copy, piece, GPSIMD_COLUMNS, PIECE)
+
             if n == 0:
-                for i in (2, 3):
-                    w_turn(i)
-                    w_copy(i)
-                s2_mm(UNITS[n], 1)
-                violation(UNITS[n], 1)
-            for g, j in AT.get(n, []):
+                w_turn(2)
+                w_turn(3)
+            turned = take(slots_to_turn, 2 if n >= 1 else 0)
+            for g, j in turned:
                 at_turn(g, j)
-            if n > 0:
-                s2_mm(UNITS[n], 1)
-            for g, j in AT.get(n, []):
+            s2_mm(unit, 1)
+            for g, j in turned:
                 at_copy(g, j)
-            if n > 0:
-                violation(UNITS[n], 1)
-            if n == 15:
-                lam_turn(UNITS[n])
-            elif n + 1 >= 11:
+            violation(unit, 1)
+            if n == STEPS - 1:
+                lam_turn(n)
+            elif n + 1 >= FIRST_SORTED_STEP:
                 lam_sort(UNITS[n + 1])
             if n >= 1:
                 mu_add(UNITS[n - 1])
-            for tile, hh in S1.get(n, []):
-                w_add(tile, hh)
-                if hh == 1 and tile + 3 < 8:
-                    load_x0(tile + 3)
-            for i, h in S3.get(n, []):
-                s3_mm(i, h, range(4))
-            for i, h in to_round:
+            for i, h in summed:
+                w_add(i, h)
+                if (i, h) == (4, 1):
+                    load_x0(7)
+
+            multiplied = take(third_products, 0 if n < 8 else 1 if n < 12 else 2)
+            for i, h in multiplied:
+                s3_mm(i, h)
+            to_turn, rounded = rounded, []
+            for i, h in scaled:
                 y_round(i, h)
                 if i % 2 == 1:
-                    to_turn.append((i // 2, h))
-            to_round = []
-            if n >= 1 and not S1.get(n):
-                pass
+                    rounded.append((i // 2, h))
             if n >= 1:
                 mu_cut(UNITS[n - 1])
-            for pair, h in to_quant:
-                y_quant(pair, h)
+            for ch, h in copied:
+                y_quant(ch, h)
                 if h == 1:
-                    codes_store(pair)
-                if (pair, h) == (1, 1):
-                    plane_store(0, nc.sync)
-            to_quant = []
-            for piece, eng in WEAVE.get(n, []):
-                if eng != "G":
-                    a_weave(piece, eng)
-            if n in WQ:
-                w_quant(WQ[n])
-            if n < 15:
-                lam_turn(UNITS[n])
-            for g, j in AT_LATE.get(n, []):
+                    codes_store(ch)
+            if n == 0:
+                shared_woven = [1]
+                shared_piece(1)
+                weave(nc.vector.tensor_copy, 1, 0, PIECE)
+            own_woven[n] = take(scalar_pieces, 1 if n >= FIRST_SCALAR_PIECE_STEP else 0)
+            for piece in own_woven[n]:
+                own_piece(piece)
+                weave(nc.scalar.copy, piece, 0, PIECE)
+            if n in (0, 6, 10):
+                w_quant(n // 4 + 1)
+            if n < STEPS - 1:
+                lam_turn(n)
+            late = take(slots_to_turn, 1 if n <= 1 else 0)
+            for g, j in late:
                 at_turn(g, j)
                 at_copy(g, j)
+            turned = turned + late
             if n in (2, 3, 6, 7):
-                load_lam(LAM.pop(0))
-            if n > 0 and n in WT:
-                w_turn(WT[n])
-                w_copy(WT[n])
-            for pair, h in to_turn:
-                y_turn(2 * pair, h)
-                y_turn(2 * pair + 1, h)
-                y_copy(pair, h)
-                to_quant.append((pair, h))
-            to_turn = []
+                load_lam(lam_to_load.pop(0))
+            if n in (3, 5, 7, 9):
+                w_turn(4 + (n - 3) // 2)
+            for ch, h in to_turn:
+                y_turn_chunk(ch, h)
+            copied = to_turn
 
-        mu_quant(14)
-        mu_add(15)
+        mu_quant(UNITS[-2])
+        mu_add(UNITS[-1])
         y_scale(4, 1)
-        mu_cut(15)
+        mu_cut(UNITS[-1])
         y_scale(5, 1)
-        mu_quant(15)
+        mu_quant(UNITS[-1])
         y_store(2, 1)
         y_round(4, 1)
         y_round(5, 1)
-        for pair, h in to_quant:
-            y_quant(pair, h)
-        for i, h in [(6, 0), (7, 0), (6, 1)]:
-            s3_mm(i, h, range(4))
-            y_scale(i, h)
-            y_round(i, h)
-            if (i, h) == (7, 0):
-                y_store(3, 0)
-                y_turn(4, 1)
-                y_turn(5, 1)
-                y_copy(2, 1)
-        y_quant(2, 1)
+        y_quant(1, 1)
+        codes_store(1)
+        plane_store(0, nc.sync)
+        for i in (6, 7):
+            s3_mm(i, 0)
+            y_scale(i, 0)
+            y_round(i, 0)
+        y_store(3, 0)
+        for h in range(HALVES):
+            y_turn_chunk(2, h)
+        s3_mm(6, 1)
+        y_scale(6, 1)
+        y_round(6, 1)
+        for h in range(HALVES):
+            y_quant(2, h)
         codes_store(2)
         y_store_tile(6, 1)
-        s3_mm(7, 1, range(4))
-        for i, h in [(6, 0), (7, 0), (6, 1)]:
-            y_turn(i, h)
+        s3_mm(7, 1)
+        y_turn(6, 0)
+        y_turn(7, 0)
+        y_turn(6, 1)
         y_copy(3, 0)
         y_scale_round(7, 1)
         y_scale(7, 1)
         y_store_tile(7, 1)
         y_turn(7, 1)
         y_copy(3, 1)
-        y_quant(3, 0)
-        codes_store_half(3, 0)
-        y_quant(3, 1)
-        codes_store_half(3, 1)
+        for h in range(HALVES):
+            y_quant(3, h)
+            codes_store_half(3, h)
         plane_store(1, nc.scalar)

from contextlib import ExitStack

import concourse.mybir as mybir
from concourse.masks import make_identity

R, Z, N, C = 1024, 512, 1024, 2048
FLOPS = 2 * R * Z * N + 2 * 2 * R * N * C

F32 = mybir.dt.float32
BF16 = mybir.dt.bfloat16
I32 = mybir.dt.int32
U32 = mybir.dt.uint32
U8 = mybir.dt.uint8
FP8X4 = mybir.dt.float8_e4m3fn_x4
FP4X4 = mybir.dt.float4_e2m1fn_x4
ALU = mybir.AluOpType
ACT = mybir.ActivationFunctionType

P = 128
K = 512
CHUNK = 2 * P
HALVES = N // K
GROUPS = C // K
STEPS = (R // CHUNK) * GROUPS
PIECE = 256
ROTATING_BANKS = 6

UNITS = [GROUPS * ch + g for g in range(GROUPS) for ch in range(2)] + list(range(2 * GROUPS, STEPS))

GPSIMD_COLUMNS = 176
FIRST_SORTED_STEP = 11
FIRST_SCALAR_PIECE_STEP = 5


def tile_augmented_lagrangian_inequality_grad_k1_kernel(
    tc, z_words, z_scales, B_words, B_scales, x0, A, b, lam, rho, d, out_0, out_1, out_2
):
    nc = tc.nc
    with ExitStack() as ctx:
        keep = ctx.enter_context(tc.tile_pool(name="keep", bufs=1))
        ring = ctx.enter_context(tc.tile_pool(name="ring", bufs=2))
        psum = ctx.enter_context(tc.psum_pool(name="psum", bufs=1))
        ctx.enter_context(tc.manual_schedule())

        t = {}
        banks_taken = [0]

        def next_bank():
            tag = "bank%d" % (banks_taken[0] % ROTATING_BANKS)
            banks_taken[0] = banks_taken[0] + 1
            return psum.tile([P, K], F32, name=tag, tag=tag)

        def kept(name, shape, dtype):
            return keep.tile(shape, dtype, name=name, tag=name, align_bytes=64)

        def ringed(name, shape, dtype, bufs):
            return ring.tile(shape, dtype, name=name, tag=name, bufs=bufs, align_bytes=64)

        def quantize(codes, plane, values):
            nc.vector.quantize_mx(out=codes.bitcast(FP8X4), scales=plane, in_=values)

        ident = kept("ident", [P, P], F32)
        z_plane = kept("z_plane", [P, R], U8)
        b_codes = kept("b_codes", [P, 2 * N], U8)
        b_plane = kept("b_plane", [P, N], U8)
        rho_bf = kept("rho_bf", [P, 4 * GROUPS], BF16)
        bound_bf = kept("bound_bf", [P, 4 * GROUPS], BF16)
        rho_f = kept("rho_f", [P, 4 * GROUPS], F32)
        shift = kept("shift", [P, 4 * GROUPS], F32)
        d_row = kept("d_row", [P, N], BF16)
        warm = kept("warm", [P, 8], F32)

        def load_plane(plane, rows, quadrants):
            for q in quadrants:
                nc.sync.dma_start(
                    out=plane[32 * q : 32 * q + 4, :].bitcast(I32), in_=rows[0, 4 * q : 4 * q + 4, :].bitcast(I32)
                )

        def load_z(half):
            t["z", half] = kept("z_codes%d" % half, [P, K], U32)
            src = z_words[0, :, K * half : K * (half + 1), :].rearrange("p n t -> p (n t)")
            nc.sync.dma_start(out=t["z", half][:].bitcast(I32), in_=src.bitcast(I32))

        def load_a(g, first_slot, slots):
            if first_slot == 0:
                t["a", g] = kept("a_raw%d" % g, [P, 4 * N], BF16)
            cols = slice(N * first_slot, N * (first_slot + slots))
            rows = A[K * g : K * (g + 1), :].rearrange("(p j) n -> p (j n)", j=4)
            nc.sync.dma_start(out=t["a", g][:, cols], in_=rows[:, cols])

        def load_x0(i):
            t["x0", i] = ringed("x0", [P, N], BF16, 5)
            nc.sync.dma_start(out=t["x0", i][:], in_=x0[P * i : P * (i + 1), :])

        def load_lam(unit):
            ch, g = divmod(unit, GROUPS)
            t["lam", unit // 2] = ringed("lam", [P, 4 * K], BF16, 4)
            rows = lam[CHUNK * ch : CHUNK * (ch + 1), K * g : K * (g + 2)].rearrange("(i p) c -> p i c", p=P)
            nc.sync.dma_start(out=t["lam", unit // 2][:].rearrange("p (i c) -> p i c", i=2), in_=rows)

        def load_by_slot(tile, vector):
            nc.sync.dma_start(
                out=tile[:].rearrange("p (g j) -> p g j", j=4), in_=vector.rearrange("(g p j) -> p g j", p=P, j=4)
            )

        def at_turn(g, j):
            words = t["a", g][:].bitcast(F32)
            bank = t["at_bank", g, j] = next_bank()
            for h in range(HALVES):
                for u in range(2):
                    first = K * j + 256 * h
                    nc.tensor.transpose(
                        bank[:, P * (2 * h + u) : P * (2 * h + u + 1)], words[:, first + u : first + 256 : 2], ident[:]
                    )

        def at_copy(g, j):
            t["at_bf", g, j] = ringed("at_bf", [P, K], F32, 4)
            nc.scalar.copy(
                out=t["at_bf", g, j][:].rearrange("p (h c u) -> p h c u", h=2, u=2),
                in_=t["at_bank", g, j][:].rearrange("p (h u c) -> p h c u", h=2, u=2),
            )

        def at_quant(g, j):
            t["at_codes", g, j] = kept("at_codes%d_%d" % (g, j), [P, HALVES * P], U32)
            t["at_plane", g, j] = kept("at_plane%d_%d" % (g, j), [P, HALVES * P], U8)
            quantize(t["at_codes", g, j][:], t["at_plane", g, j][:], t["at_bf", g, j][:].bitcast(BF16))

        def piece_views(piece, lo, hi):
            h, g, part = piece // 8, piece % 8 // 2, piece % 2
            first = K * h + PIECE * part
            src = t["a", g][:].rearrange("p (j n) -> p j n", j=4)[:, :, first + lo : first + hi]
            return t["a_bf", piece][:, 4 * lo : 4 * hi], src

        def weave(copy, piece, lo, hi):
            dst, src = piece_views(piece, lo, hi)
            copy(out=dst.rearrange("p (c i j) -> p c j i", i=4, j=4), in_=src.rearrange("p j (c i) -> p c j i", i=4))

        def weave_gpsimd(piece):
            dst, src = piece_views(piece, 0, GPSIMD_COLUMNS)
            nc.gpsimd.tensor_scalar(
                out=dst.rearrange("p (n j) -> p n j", j=4),
                in0=src.rearrange("p j n -> p n j"),
                scalar1=1.0,
                scalar2=0.0,
                op0=ALU.mult,
                op1=ALU.add,
            )

        def own_piece(piece):
            t["a_bf", piece] = ringed("a_bf", [P, 4 * PIECE], BF16, 3)

        def shared_piece(piece):
            t["a_bf", piece] = ringed("a_bf_shared", [P, 4 * PIECE], BF16, 1)

        def a_quant(piece):
            h, g, part = piece // 8, piece % 8 // 2, piece % 2
            if part == 0:
                t["a_codes", g, h] = kept("a_codes%d_%d" % (g, h), [P, K], U32)
                t["a_plane", g, h] = kept("a_plane%d_%d" % (g, h), [P, K], U8)
            cols = slice(PIECE * part, PIECE * (part + 1))
            quantize(t["a_codes", g, h][:, cols], t["a_plane", g, h][:, cols], t["a_bf", piece][:])

        def s1_mm(i, h):
            bank = t["s1", i, h] = next_bank()
            nc.tensor.matmul_mx(
                out=bank[:],
                lhsT=t["z", i // 4][:, P * (i % 4) : P * (i % 4 + 1)].bitcast(FP8X4),
                lhsT_scale=z_plane[:, P * i : P * (i + 1)],
                rhs=b_codes[:, 2 * K * h : 2 * K * (h + 1)].bitcast(FP4X4),
                rhs_scale=b_plane[:, K * h : K * (h + 1)],
                start=True,
                stop=True,
            )

        def w_add(i, h):
            if h == 0:
                t["w_rows", i] = ringed("w_rows", [P, N], BF16, 3)
            nc.vector.tensor_tensor(
                out=t["w_rows", i][:, K * h : K * (h + 1)].rearrange("r (u p e) -> r u p e", u=2, e=2),
                in0=t["s1", i, h][:].rearrange("r (p u e) -> r u p e", u=2, e=2),
                in1=t["x0", i][:, K * h : K * (h + 1)].rearrange("r (p u e) -> r u p e", u=2, e=2),
                op=ALU.add,
            )

        def w_turn(i):
            words = t["w_rows", i][:].bitcast(F32)
            bank = next_bank()
            for q in range(4):
                nc.tensor.transpose(bank[:, P * q : P * (q + 1)], words[:, P * q : P * (q + 1)], ident[:])
            if i % 2 == 0:
                t["w_turned", i // 2] = ringed("w_turned", [P, 2 * K], F32, 2)
            dst = t["w_turned", i // 2][:].rearrange("p (h i r u) -> p i h r u", h=2, i=2, u=2)
            nc.scalar.copy(out=dst[:, i % 2], in_=bank[:].rearrange("p (h u r) -> p h r u", h=2, u=2))

        def w_quant(ch):
            t["w_codes", ch] = kept("w_codes%d" % ch, [P, HALVES * CHUNK], U32)
            t["w_plane", ch] = kept("w_plane%d" % ch, [P, HALVES * CHUNK], U8)
            quantize(t["w_codes", ch][:], t["w_plane", ch][:], t["w_turned", ch][:].bitcast(BF16))

        def s2_mm(unit, u):
            ch, g = divmod(unit, GROUPS)
            bank = t["s2", unit, u] = next_bank()
            for e in range(2):
                for h in range(HALVES):
                    cols = slice(P * h, P * (h + 1))
                    points = slice(CHUNK * h, CHUNK * (h + 1))
                    nc.tensor.matmul_mx(
                        out=bank[:, CHUNK * e : CHUNK * (e + 1)],
                        lhsT=t["at_codes", g, 2 * u + e][:, cols].bitcast(FP8X4),
                        lhsT_scale=t["at_plane", g, 2 * u + e][:, cols],
                        rhs=t["w_codes", ch][:, points].bitcast(FP8X4),
                        rhs_scale=t["w_plane", ch][:, points],
                        start=(h == 0),
                        stop=(h == HALVES - 1),
                    )

        def violation(unit, u):
            g = unit % GROUPS
            if u == 0:
                t["viol", unit] = ringed("viol", [P, 4, CHUNK], F32, 3)
            for e in range(2):
                j = 2 * u + e
                nc.scalar.activation(
                    out=t["viol", unit][:, j, :],
                    in_=t["s2", unit, u][:, CHUNK * e : CHUNK * (e + 1)],
                    func=ACT.Identity,
                    bias=shift[:, 4 * g + j : 4 * g + j + 1],
                    scale=rho_f[:, 4 * g + j : 4 * g + j + 1],
                )

        def lam_sort(unit):
            words = t["lam", unit // 2][:].bitcast(F32).rearrange("r (i g p u) -> r g u i p", i=2, g=2, u=2)
            t["lam_sorted", unit] = ringed("lam_sorted", [P, K], F32, 3)
            nc.scalar.copy(
                out=t["lam_sorted", unit][:].rearrange("r (u i p) -> r u i p", u=2, i=2), in_=words[:, unit % 2]
            )

        def lam_turn(step):
            unit = UNITS[step]
            tag = "lam_bank%d" % (step % 2)
            bank = t["lam_bank", unit] = psum.tile([P, K], F32, name=tag, tag=tag)
            for u in range(2):
                for i in range(2):
                    cols = slice(P * (2 * u + i), P * (2 * u + i + 1))
                    if step >= FIRST_SORTED_STEP:
                        src = t["lam_sorted", unit][:, cols]
                    else:
                        first = K * i + 256 * (unit % 2)
                        src = t["lam", unit // 2][:].bitcast(F32)[:, first + u : first + 256 : 2]
                    nc.tensor.transpose(bank[:, cols], src, ident[:])

        def mu_add(unit):
            t["mu_sum", unit] = ringed("mu_sum", [P, 4 * CHUNK], BF16, 2)
            nc.vector.tensor_tensor(
                out=t["mu_sum", unit][:].rearrange("p (u r e) -> p u r e", u=2, e=2),
                in0=t["lam_bank", unit][:].bitcast(BF16).rearrange("p (u r e) -> p u r e", u=2, e=2),
                in1=t["viol", unit][:].rearrange("p (u e) r -> p u r e", u=2),
                op=ALU.add,
            )

        def mu_cut(unit):
            t["mu", unit] = ringed("mu", [P, 4 * CHUNK], BF16, 2)
            nc.vector.tensor_scalar_max(
                out=t["mu", unit][:].rearrange("p (r u e) -> p r u e", u=2, e=2),
                in0=t["mu_sum", unit][:].rearrange("p (u r e) -> p r u e", u=2, e=2),
                scalar1=0.0,
            )

        def mu_quant(unit):
            t["mu_codes", unit] = kept("mu_codes%d" % unit, [P, CHUNK], U32)
            t["mu_plane", unit] = kept("mu_plane%d" % unit, [P, CHUNK], U8)
            quantize(t["mu_codes", unit][:], t["mu_plane", unit][:], t["mu", unit][:])

        def s3_mm(i, h):
            cols = slice(P * (i % 2), P * (i % 2 + 1))
            bank = t["s3", i, h] = next_bank()
            for g in range(GROUPS):
                unit = GROUPS * (i // 2) + g
                nc.tensor.matmul_mx(
                    out=bank[:],
                    lhsT=t["mu_codes", unit][:, cols].bitcast(FP8X4),
                    lhsT_scale=t["mu_plane", unit][:, cols],
                    rhs=t["a_codes", g, h][:].bitcast(FP8X4),
                    rhs_scale=t["a_plane", g, h][:],
                    start=(g == 0),
                    stop=(g == GROUPS - 1),
                )

        def y_scale(i, h):
            if i % 2 == 0:
                t["y", i // 2, h] = ringed("y", [P, 2, K], F32, 4)
            nc.vector.tensor_tensor(
                out=t["y", i // 2, h][:, i % 2, :], in0=t["s3", i, h][:], in1=d_row[:, K * h : K * (h + 1)], op=ALU.mult
            )

        def y_store(ch, h):
            dst = out_0[CHUNK * ch : CHUNK * (ch + 1), K * h : K * (h + 1)].rearrange("(i p) n -> p i n", p=P)
            nc.sync.dma_start(out=dst, in_=t["y", ch, h][:])

        def y_store_tile(i, h):
            nc.sync.dma_start(out=out_0[P * i : P * (i + 1), K * h : K * (h + 1)], in_=t["y", i // 2, h][:, i % 2, :])

        def y_round(i, h):
            t["y_rows", i, h] = ringed("y_rows", [P, K], BF16, 7)
            nc.scalar.copy(
                out=t["y_rows", i, h][:].rearrange("r (u p e) -> r u p e", u=2, e=2),
                in_=t["y", i // 2, h][:, i % 2, :].rearrange("r (p u e) -> r u p e", u=2, e=2),
            )

        def y_scale_round(i, h):
            t["y_rows", i, h] = ringed("y_rows", [P, K], BF16, 7)
            nc.vector.tensor_tensor(
                out=t["y_rows", i, h][:].rearrange("r (u p e) -> r u p e", u=2, e=2),
                in0=t["s3", i, h][:].rearrange("r (p u e) -> r u p e", u=2, e=2),
                in1=d_row[:, K * h : K * (h + 1)].rearrange("r (p u e) -> r u p e", u=2, e=2),
                op=ALU.mult,
            )

        def y_turn(i, h):
            if i % 2 == 0:
                t["y_bank", i // 2, h] = next_bank()
            words = t["y_rows", i, h][:].bitcast(F32)
            for u in range(2):
                first = P * (2 * u + i % 2)
                nc.tensor.transpose(t["y_bank", i // 2, h][:, first : first + P], words[:, P * u : P * (u + 1)], ident[:])

        def y_copy(ch, h):
            t["y_turned", ch, h] = ringed("y_turned", [P, K], F32, 3)
            nc.scalar.copy(
                out=t["y_turned", ch, h][:].rearrange("p (r u) -> p r u", u=2),
                in_=t["y_bank", ch, h][:].rearrange("p (u r) -> p r u", u=2),
            )

        def y_turn_chunk(ch, h):
            y_turn(2 * ch, h)
            y_turn(2 * ch + 1, h)
            y_copy(ch, h)

        def y_quant(ch, h):
            if h == 0:
                t["y_codes", ch] = kept("y_codes%d" % ch, [P, HALVES * CHUNK], U32)
                if ch % 2 == 0:
                    t["y_plane", ch // 2] = kept("y_plane%d" % (ch // 2), [P, HALVES * 2 * CHUNK], U8)
            first = 2 * CHUNK * h + CHUNK * (ch % 2)
            quantize(
                t["y_codes", ch][:, CHUNK * h : CHUNK * (h + 1)],
                t["y_plane", ch // 2][:, first : first + CHUNK],
                t["y_turned", ch, h][:].bitcast(BF16),
            )

        def codes_store(ch):
            dst = out_1[:, :, CHUNK * ch : CHUNK * (ch + 1), :].rearrange("h p m t -> p h (m t)")
            src = t["y_codes", ch][:].rearrange("p (h m) -> p h m", h=2)
            nc.sync.dma_start(out=dst.bitcast(I32), in_=src.bitcast(I32))

        def codes_store_half(ch, h):
            dst = out_1[h, :, CHUNK * ch : CHUNK * (ch + 1), :].rearrange("p m t -> p (m t)")
            nc.sync.dma_start(out=dst.bitcast(I32), in_=t["y_codes", ch][:, CHUNK * h : CHUNK * (h + 1)].bitcast(I32))

        def plane_store(pair, queue):
            for q in range(4):
                dst = out_2[:, 4 * q : 4 * q + 4, 2 * CHUNK * pair : 2 * CHUNK * (pair + 1)].rearrange("h q m -> q h m")
                src = t["y_plane", pair][32 * q : 32 * q + 4, :].rearrange("q (h m) -> q h m", h=2)
                queue.dma_start(out=dst.bitcast(I32), in_=src.bitcast(I32))

        nc.gpsimd.memset(z_plane[:].bitcast(I32), 0)
        nc.gpsimd.memset(b_plane[:].bitcast(I32), 0)
        make_identity(nc, ident[:])
        nc.vector.memset(warm[:], 0.0)
        nc.scalar.activation(out=warm[:, 4:5], in_=warm[:, 0:1], func=ACT.Identity)

        load_plane(z_plane, z_scales, range(3))
        load_z(0)
        nc.sync.dma_start(out=b_codes[:].bitcast(I32), in_=B_words[0].bitcast(I32))
        load_x0(0)
        load_plane(z_plane, z_scales, [3])
        load_plane(b_plane, B_scales, range(4))
        load_x0(1)
        load_a(0, 0, 2)
        load_x0(2)
        load_a(0, 2, 2)
        load_x0(3)
        load_by_slot(rho_bf, rho)
        load_by_slot(bound_bf, b)
        load_a(1, 0, 2)
        load_lam(UNITS[0])
        load_a(1, 2, 2)
        load_z(1)
        load_x0(4)
        load_lam(UNITS[1])
        load_a(2, 0, 4)
        load_lam(UNITS[4])
        load_lam(UNITS[5])
        load_a(3, 0, 4)
        nc.sync.dma_start(out=d_row[:], in_=d.partition_broadcast(P))

        for i in range(2):
            for h in range(HALVES):
                s1_mm(i, h)
            for h in range(HALVES):
                w_add(i, h)
        nc.vector.tensor_copy(out=rho_f[:], in_=rho_bf[:])
        nc.vector.scalar_tensor_tensor(
            out=shift[:], in0=bound_bf[:], scalar=-1.0, in1=rho_bf[:], op0=ALU.mult, op1=ALU.mult
        )

        def turns_then_first_product(i):
            w_turn(i)
            at_turn(0, i)
            at_copy(0, i)
            for h in range(HALVES):
                s1_mm(i + 2, h)

        turns_then_first_product(0)
        for h in range(HALVES):
            w_add(2, h)
        at_quant(0, 0)
        turns_then_first_product(1)
        w_quant(0)
        at_quant(0, 1)
        for h in range(HALVES):
            w_add(3, h)
        load_x0(5)
        load_x0(6)
        turned = [(0, 2), (0, 3)]
        for g, j in turned:
            at_turn(g, j)
        for g, j in turned:
            at_copy(g, j)
        own_piece(0)
        weave(nc.vector.tensor_copy, 0, 0, PIECE)

        slots_to_turn = [(g, j) for g in range(1, GROUPS) for j in range(4)]
        first_products = [(i, h) for i in range(4, 8) for h in range(HALVES)]
        shared_pieces = list(range(2, 8)) + list(range(12, 16))
        scalar_pieces = list(range(8, 12))
        lam_to_load = list(range(2 * GROUPS, STEPS, 2))
        third_products = [(i, h) for h in range(HALVES) for i in range(4)]
        third_products = third_products + [(i, h) for h in range(HALVES) for i in (4, 5)]

        def take(queue, count):
            return [queue.pop(0) for k in range(min(count, len(queue)))]

        own_woven = {-1: [0]}
        shared_woven = []
        multiplied, rounded, copied = [], [], []
        for n in range(STEPS):
            unit = UNITS[n]

            for g, j in turned:
                at_quant(g, j)
            for piece in own_woven.get(n - 2, []):
                a_quant(piece)
            if n >= 2:
                mu_quant(UNITS[n - 2])
            for piece in shared_woven:
                a_quant(piece)
            shared_woven = take(shared_pieces, 1 if n >= 1 else 0)
            for piece in shared_woven:
                shared_piece(piece)
                weave_gpsimd(piece)

            scaled, multiplied = multiplied, []
            for i, h in scaled:
                y_scale(i, h)
                if i % 2 == 1:
                    y_store(i // 2, h)
            summed = take(first_products, 1 if n >= 1 else 0)
            for i, h in summed:
                s1_mm(i, h)
            s2_mm(unit, 0)
            violation(unit, 0)
            for piece in shared_woven:
                weave(nc.scalar.copy, piece, GPSIMD_COLUMNS, PIECE)

            if n == 0:
                w_turn(2)
                w_turn(3)
            turned = take(slots_to_turn, 2 if n >= 1 else 0)
            for g, j in turned:
                at_turn(g, j)
            s2_mm(unit, 1)
            for g, j in turned:
                at_copy(g, j)
            violation(unit, 1)
            if n == STEPS - 1:
                lam_turn(n)
            elif n + 1 >= FIRST_SORTED_STEP:
                lam_sort(UNITS[n + 1])
            if n >= 1:
                mu_add(UNITS[n - 1])
            for i, h in summed:
                w_add(i, h)
                if (i, h) == (4, 1):
                    load_x0(7)

            multiplied = take(third_products, 0 if n < 8 else 1 if n < 12 else 2)
            for i, h in multiplied:
                s3_mm(i, h)
            to_turn, rounded = rounded, []
            for i, h in scaled:
                y_round(i, h)
                if i % 2 == 1:
                    rounded.append((i // 2, h))
            if n >= 1:
                mu_cut(UNITS[n - 1])
            for ch, h in copied:
                y_quant(ch, h)
                if h == 1:
                    codes_store(ch)
            if n == 0:
                shared_woven = [1]
                shared_piece(1)
                weave(nc.vector.tensor_copy, 1, 0, PIECE)
            own_woven[n] = take(scalar_pieces, 1 if n >= FIRST_SCALAR_PIECE_STEP else 0)
            for piece in own_woven[n]:
                own_piece(piece)
                weave(nc.scalar.copy, piece, 0, PIECE)
            if n in (0, 6, 10):
                w_quant(n // 4 + 1)
            if n < STEPS - 1:
                lam_turn(n)
            late = take(slots_to_turn, 1 if n <= 1 else 0)
            for g, j in late:
                at_turn(g, j)
                at_copy(g, j)
            turned = turned + late
            if n in (2, 3, 6, 7):
                load_lam(lam_to_load.pop(0))
            if n in (3, 5, 7, 9):
                w_turn(4 + (n - 3) // 2)
            for ch, h in to_turn:
                y_turn_chunk(ch, h)
            copied = to_turn

        mu_quant(UNITS[-2])
        mu_add(UNITS[-1])
        y_scale(4, 1)
        mu_cut(UNITS[-1])
        y_scale(5, 1)
        mu_quant(UNITS[-1])
        y_store(2, 1)
        y_round(4, 1)
        y_round(5, 1)
        y_quant(1, 1)
        codes_store(1)
        plane_store(0, nc.sync)
        for i in (6, 7):
            s3_mm(i, 0)
            y_scale(i, 0)
            y_round(i, 0)
        y_store(3, 0)
        for h in range(HALVES):
            y_turn_chunk(2, h)
        s3_mm(6, 1)
        y_scale(6, 1)
        y_round(6, 1)
        for h in range(HALVES):
            y_quant(2, h)
        codes_store(2)
        y_store_tile(6, 1)
        s3_mm(7, 1)
        y_turn(6, 0)
        y_turn(7, 0)
        y_turn(6, 1)
        y_copy(3, 0)
        y_scale_round(7, 1)
        y_scale(7, 1)
        y_store_tile(7, 1)
        y_turn(7, 1)
        y_copy(3, 1)
        for h in range(HALVES):
            y_quant(3, h)
            codes_store_half(3, h)
        plane_store(1, nc.scalar)
